import numpy as np
import ml_dtypes


def mxq(x, axis, fmt="e4m3"):
    dtype, down = {"e4m3": (ml_dtypes.float8_e4m3fn, 7), "e5m2": (ml_dtypes.float8_e5m2, 14)}[fmt]
    v = np.moveaxis(np.asarray(x, np.float32).astype(ml_dtypes.bfloat16).astype(np.float64), axis, -1)
    blocks = v.reshape(v.shape[:-1] + (-1, 32))
    amax = np.abs(blocks).max(-1, keepdims=True)
    byte = np.maximum(np.where(amax > 0, np.frexp(amax)[1] - 1 + 127, 0) - down, 1)
    scale = np.exp2(byte - 127.0)
    codes = (blocks / scale).astype(np.float32).astype(dtype).astype(np.float64)
    return np.moveaxis((codes * scale).reshape(v.shape), -1, axis)


WIDE = False


def mx_kscale(k):
    if not WIDE:
        return np.ones(k)
    levels = np.array([10, -10, 5, -5, 0])
    if k % 512:
        return np.exp2(np.random.permutation(np.resize(levels, k // 32))).repeat(32)
    a = np.empty((k // 512, 16))
    for p in range(k // 512):
        a[p, :8] = np.random.permutation(np.resize(levels, 8))
        for g in range(8):
            far = levels[np.abs(levels - a[p, g]) >= 10]
            a[p, g + 8] = far[np.random.randint(len(far))]
    return np.exp2(a.ravel()).repeat(32)


def f64(x):
    return np.asarray(x).astype(np.float64)


def striped(idx):
    return np.tile(np.asarray(idx).reshape(-1, 16).T, (8, 1)).astype(np.uint16)


def unstriped(offs):
    return offs[:16].T.reshape(-1).astype(np.int64)


E2M1 = np.array([0.0, 0.5, 1.0, 1.5, 2.0, 3.0, 4.0, 6.0, -0.0, -0.5, -1.0, -1.5, -2.0, -3.0, -4.0, -6.0])


def pack_weight(w, fmt):
    k, n = w.shape
    w = f64(np.asarray(w, np.float32).astype(ml_dtypes.bfloat16)).reshape(k // 32, 32, n)
    amax = np.abs(w).max(1)
    if fmt == "e4m3":
        byte = np.frexp(amax)[1] - 1 + 127 - 7
    else:
        mant, ex = np.frexp(amax / 6.0)
        byte = np.where(mant > 0.5, ex, ex - 1) + 127
    byte = np.clip(np.where(amax > 0, byte, 1), 1, 254)
    scaled = (w * np.exp2(127.0 - byte)[:, None, :]).reshape(k, n).astype(np.float32)
    by_word = np.ascontiguousarray(scaled.reshape(k // 512, 128, 4, n).transpose(0, 1, 3, 2))
    if fmt == "e4m3":
        words = by_word.astype(ml_dtypes.float8_e4m3fn).view(np.uint8)
    else:
        c = by_word.astype(ml_dtypes.float4_e2m1fn).view(np.uint8) & 0xF
        words = (c[..., 0::2] | (c[..., 1::2] << 4)).reshape(k // 512, 128, 2 * n)
    return np.ascontiguousarray(words), np.ascontiguousarray(byte.astype(np.uint8).reshape(k // 512, 16, n))


def unpack_weight(words, scales, fmt):
    g, _, n = scales.shape
    words = np.ascontiguousarray(words).reshape(g, 128, n, -1)
    if fmt == "e4m3":
        vals = words.view(ml_dtypes.float8_e4m3fn).astype(np.float64)
    else:
        nib = np.empty((g, 128, n, 4), np.uint8)
        nib[..., 0::2] = words & 0xF
        nib[..., 1::2] = words >> 4
        vals = E2M1[nib]
    vals = vals * np.repeat(np.exp2(scales.astype(np.float64) - 127.0), 8, axis=1)[..., None]
    return vals.transpose(0, 1, 3, 2).reshape(g * 512, n)


B, N, T, D, DV, NQ = 1, 512, 2048, 256, 512, 512


def setup_inputs():
    n = np.random.standard_normal
    idx = np.random.permutation(T)[:B * N]
    s = mx_kscale(DV)[:, None]
    z = mx_kscale(NQ)[:, None]
    p = np.exp(n((B, NQ, N)))
    p = p / p.mean(2, keepdims=True)
    kp = pack_weight(n((DV, T)) / s, "e4m3")
    return {
        "doT": (n((B, DV, NQ)) * s / np.sqrt(DV)).astype(np.float32),
        "v_words": kp[0],
        "v_scales": kp[1],
        "p": (p * z / np.sqrt(NQ)).astype(np.float32),
        "delta": (0.3 * n((B, NQ, 1))).astype(np.float32),
        "qm": (n((B, NQ, D)) / z).astype(np.float32),
        "offs": striped(idx),
    }


def reference(doT, v_words, v_scales, p, delta, qm, offs):
    idx = unstriped(offs)
    pool = unpack_weight(v_words, v_scales, "e4m3")
    pick = lambda x: x[:, idx].reshape(x.shape[0], B, N).transpose(1, 0, 2)
    dp = mxq(f64(doT), 1, "e4m3").transpose(0, 2, 1) @ pick(pool)
    ds = f64(p) * (dp - f64(delta))
    dk = mxq(f64(qm), 1, "e4m3").transpose(0, 2, 1) @ mxq(ds, 1, "e4m3")
    out = np.zeros((D, T))
    out[:, idx] = dk.transpose(1, 0, 2).reshape(D, B * N)
    return out

@@ -1,0 +1,134 @@
+from contextlib import ExitStack
+
+import concourse.mybir as mybir
+
+NQ, N, T, D, DV = 512, 512, 2048, 256, 512
+FLOPS = 2 * DV * NQ * N + 2 * NQ * D * N
+
+F32 = mybir.dt.float32
+BF16 = mybir.dt.bfloat16
+I32 = mybir.dt.int32
+U32 = mybir.dt.uint32
+U16 = mybir.dt.uint16
+U8 = mybir.dt.uint8
+FP8X4 = mybir.dt.float8_e4m3fn_x4
+IDENTITY = mybir.ActivationFunctionType.Identity
+MULT = mybir.AluOpType.mult
+
+P = 128
+PACK = 4
+HALF = N // 2
+LIST_COLS = N // 16
+
+
+def tile_attend_bwd_kernel(tc, doT, v_words, v_scales, p, delta, qm, offs, out):
+    nc = tc.nc
+    with ExitStack() as ctx:
+        sb = ctx.enter_context(tc.tile_pool(name="sb", bufs=1))
+        ps = ctx.enter_context(tc.psum_pool(name="ps", bufs=1))
+
+        offsets = sb.tile([P, LIST_COLS], U16, name="offsets")
+        pool_scales = sb.tile([P, T // 4], I32, name="pool_scales")
+        pool_words = sb.tile([P, T], I32, name="pool_words")
+        do_raw = sb.tile([P, PACK, NQ], F32, name="do_raw")
+        qm_raw = sb.tile([P, PACK, D], F32, name="qm_raw")
+        p_raw = [sb.tile([P, PACK, HALF], F32, name=f"p_raw{h}") for h in range(2)]
+        delta_raw = sb.tile([P, PACK], F32, name="delta_raw")
+        neg_delta = sb.tile([P, PACK], F32, name="neg_delta")
+        windows = [sb.tile([P, T], F32, name=f"window{c}") for c in range(2)]
+
+        def list_half(h):
+            return offsets[:, h * (LIST_COLS // 2) : (h + 1) * (LIST_COLS // 2)]
+
+        nc.vector.memset(pool_scales[:], 0)
+        nc.sync.dma_start(offsets[:], offs)
+        nc.sync.dma_start(delta_raw[:], delta[0].rearrange("(p t) o -> p (t o)", t=PACK))
+        nc.sync.dma_start(do_raw[:], doT[0].rearrange("(p j) q -> p j q", j=PACK))
+        scale_rows = v_scales[0].bitcast(I32)
+        for quad in range(4):
+            nc.scalar.dma_start(pool_scales[32 * quad : 32 * quad + 4, :], scale_rows[4 * quad : 4 * quad + 4, :])
+        nc.sync.dma_start(pool_words[:], v_words[0].rearrange("p n r -> p (n r)").bitcast(I32))
+        nc.sync.dma_start(qm_raw[:], qm[0].rearrange("(p t) d -> p t d", t=PACK))
+        p_rows = p[0].rearrange("(p t) n -> p t n", t=PACK)
+        for h in range(2):
+            nc.sync.dma_start(p_raw[h][:], p_rows[:, :, h * HALF : (h + 1) * HALF])
+
+        for c in range(2):
+            nc.vector.memset(windows[c][:], 0.0)
+        nc.scalar.activation(neg_delta[:], delta_raw[:], IDENTITY, scale=-1.0)
+
+        v_sc = sb.tile([P, N], U8, name="v_sc", align_bytes=64)
+        nc.vector.tensor_copy(v_sc[:], pool_scales[:].bitcast(U8).indirect(offsets[:]))
+
+        do_codes, do_sc = [], []
+        do_src = do_raw[:].rearrange("p j (m u e) -> p u m j e", u=2, e=2)
+        do_bf = [sb.tile([P, 2, P, PACK], BF16, name=f"do_bf{u}", align_bytes=64) for u in range(2)]
+        nc.vector.tensor_copy(do_bf[0][:].rearrange("p e m j -> p m j e"), do_src[:, 0])
+        nc.scalar.copy(do_bf[1][:].rearrange("p e m j -> p m j e"), do_src[:, 1])
+        for u in range(2):
+            codes = sb.tile([P, 2 * P], U32, name=f"do_codes{u}", align_bytes=64)
+            sc = sb.tile([P, 2 * P], U8, name=f"do_sc{u}", align_bytes=64)
+            nc.vector.quantize_mx(codes[:].bitcast(FP8X4), sc[:], do_bf[u][:].rearrange("p e m j -> p (e m j)"))
+            do_codes.append(codes)
+            do_sc.append(sc)
+
+        centred = []
+        for h in range(2):
+            v_codes = sb.tile([P, HALF], U32, name=f"v_codes{h}", align_bytes=64)
+            nc.vector.tensor_copy(v_codes[:], pool_words[:].bitcast(U32).indirect(list_half(h)))
+            cen = sb.tile([P, PACK, HALF], F32, name=f"centred{h}")
+            for u in range(2):
+                dp = ps.tile([P, 2, HALF], F32, name=f"dp{h}{u}")
+                for e in range(2):
+                    nc.tensor.matmul_mx(
+                        dp[:, e, :],
+                        lhsT=do_codes[u][:, e * P : (e + 1) * P].bitcast(FP8X4),
+                        lhsT_scale=do_sc[u][:, e * P : (e + 1) * P],
+                        rhs=v_codes[:].bitcast(FP8X4),
+                        rhs_scale=v_sc[:, h * HALF : (h + 1) * HALF],
+                        start=True,
+                        stop=True,
+                    )
+                for e in range(2):
+                    t = 2 * u + e
+                    nc.scalar.activation(cen[:, t, :], dp[:, e, :], IDENTITY, bias=neg_delta[:, t : t + 1])
+            centred.append(cen)
+
+        qm_bf = sb.tile([P, D, PACK], BF16, name="qm_bf", align_bytes=64)
+        nc.vector.tensor_copy(
+            qm_bf[:].rearrange("p (c i) t -> p c t i", i=2), qm_raw[:].rearrange("p t (c i) -> p c t i", i=2)
+        )
+        qm_codes = sb.tile([P, D], U32, name="qm_codes", align_bytes=64)
+        qm_sc = sb.tile([P, D], U8, name="qm_sc", align_bytes=64)
+        nc.vector.quantize_mx(qm_codes[:].bitcast(FP8X4), qm_sc[:], qm_bf[:].rearrange("p d t -> p (d t)"))
+
+        dk = [sb.tile([P, N], F32, name=f"dk{c}") for c in range(2)]
+        for h in range(2):
+            ds_bf = sb.tile([P, HALF, PACK], BF16, name=f"ds_bf{h}", align_bytes=64)
+            nc.vector.tensor_tensor(
+                ds_bf[:].rearrange("p (c i) t -> p c t i", i=2),
+                centred[h][:].rearrange("p t (c i) -> p c t i", i=2),
+                p_raw[h][:].rearrange("p t (c i) -> p c t i", i=2),
+                MULT,
+            )
+            ds_codes = sb.tile([P, HALF], U32, name=f"ds_codes{h}", align_bytes=64)
+            ds_sc = sb.tile([P, HALF], U8, name=f"ds_sc{h}", align_bytes=64)
+            nc.vector.quantize_mx(ds_codes[:].bitcast(FP8X4), ds_sc[:], ds_bf[:].rearrange("p n t -> p (n t)"))
+            for c in range(2):
+                acc = ps.tile([P, HALF], F32, name=f"dk_acc{h}{c}")
+                nc.tensor.matmul_mx(
+                    acc[:],
+                    lhsT=qm_codes[:, c * P : (c + 1) * P].bitcast(FP8X4),
+                    lhsT_scale=qm_sc[:, c * P : (c + 1) * P],
+                    rhs=ds_codes[:].bitcast(FP8X4),
+                    rhs_scale=ds_sc[:],
+                    start=True,
+                    stop=True,
+                )
+                nc.scalar.copy(dk[c][:, h * HALF : (h + 1) * HALF], acc[:])
+
+        for h in range(2):
+            nc.vector.tensor_copy(windows[0][:].indirect(list_half(h)), dk[0][:, h * HALF : (h + 1) * HALF])
+        nc.sync.dma_start(out[0:P, :], windows[0][:])
+        nc.vector.tensor_copy(windows[1][:].indirect(offsets[:]), dk[1][:])
+        nc.sync.dma_start(out[P : 2 * P, :], windows[1][:])

@@ -40,25 +40,23 @@ def tile_attend_bwd_kernel(tc, doT, v_words, v_scales, p, delta, qm, offs, out):
         def list_half(h):
             return offsets[:, h * (LIST_COLS // 2) : (h + 1) * (LIST_COLS // 2)]
 
-        nc.vector.memset(pool_scales[:], 0)
+        nc.vector.memset(pool_scales[:, 0 : T // 8], 0)
+        nc.gpsimd.memset(pool_scales[:, T // 8 : T // 4], 0)
+        nc.sync.dma_start(do_raw[:], doT[0].rearrange("(p j) q -> p j q", j=PACK))
         nc.sync.dma_start(offsets[:], offs)
         nc.sync.dma_start(delta_raw[:], delta[0].rearrange("(p t) o -> p (t o)", t=PACK))
-        nc.sync.dma_start(do_raw[:], doT[0].rearrange("(p j) q -> p j q", j=PACK))
         scale_rows = v_scales[0].bitcast(I32)
         for quad in range(4):
-            nc.scalar.dma_start(pool_scales[32 * quad : 32 * quad + 4, :], scale_rows[4 * quad : 4 * quad + 4, :])
+            nc.sync.dma_start(pool_scales[32 * quad : 32 * quad + 4, :], scale_rows[4 * quad : 4 * quad + 4, :])
         nc.sync.dma_start(pool_words[:], v_words[0].rearrange("p n r -> p (n r)").bitcast(I32))
         nc.sync.dma_start(qm_raw[:], qm[0].rearrange("(p t) d -> p t d", t=PACK))
         p_rows = p[0].rearrange("(p t) n -> p t n", t=PACK)
         for h in range(2):
             nc.sync.dma_start(p_raw[h][:], p_rows[:, :, h * HALF : (h + 1) * HALF])
 
-        for c in range(2):
-            nc.vector.memset(windows[c][:], 0.0)
+        nc.vector.memset(windows[0][:].bitcast(I32), 0)
+        nc.gpsimd.memset(windows[1][:].bitcast(I32), 0)
         nc.scalar.activation(neg_delta[:], delta_raw[:], IDENTITY, scale=-1.0)
-
-        v_sc = sb.tile([P, N], U8, name="v_sc", align_bytes=64)
-        nc.vector.tensor_copy(v_sc[:], pool_scales[:].bitcast(U8).indirect(offsets[:]))
 
         do_codes, do_sc = [], []
         do_src = do_raw[:].rearrange("p j (m u e) -> p u m j e", u=2, e=2)
@@ -72,63 +70,75 @@ def tile_attend_bwd_kernel(tc, doT, v_words, v_scales, p, delta, qm, offs, out):
             do_codes.append(codes)
             do_sc.append(sc)
 
+        v_sc = sb.tile([P, N], U8, name="v_sc", align_bytes=64)
+        nc.vector.tensor_copy(v_sc[:], pool_scales[:].bitcast(U8).indirect(offsets[:]))
+
         centred = []
         for h in range(2):
             v_codes = sb.tile([P, HALF], U32, name=f"v_codes{h}", align_bytes=64)
             nc.vector.tensor_copy(v_codes[:], pool_words[:].bitcast(U32).indirect(list_half(h)))
             cen = sb.tile([P, PACK, HALF], F32, name=f"centred{h}")
-            for u in range(2):
-                dp = ps.tile([P, 2, HALF], F32, name=f"dp{h}{u}")
-                for e in range(2):
-                    nc.tensor.matmul_mx(
-                        dp[:, e, :],
-                        lhsT=do_codes[u][:, e * P : (e + 1) * P].bitcast(FP8X4),
-                        lhsT_scale=do_sc[u][:, e * P : (e + 1) * P],
-                        rhs=v_codes[:].bitcast(FP8X4),
-                        rhs_scale=v_sc[:, h * HALF : (h + 1) * HALF],
-                        start=True,
-                        stop=True,
-                    )
-                for e in range(2):
-                    t = 2 * u + e
-                    nc.scalar.activation(cen[:, t, :], dp[:, e, :], IDENTITY, bias=neg_delta[:, t : t + 1])
+            for t in range(PACK):
+                u, e = divmod(t, 2)
+                dp = ps.tile([P, HALF], F32, name=f"bank{PACK * h + t}")
+                nc.tensor.matmul_mx(
+                    dp[:],
+                    lhsT=do_codes[u][:, e * P : (e + 1) * P].bitcast(FP8X4),
+                    lhsT_scale=do_sc[u][:, e * P : (e + 1) * P],
+                    rhs=v_codes[:].bitcast(FP8X4),
+                    rhs_scale=v_sc[:, h * HALF : (h + 1) * HALF],
+                    start=True,
+                    stop=True,
+                )
+                nc.scalar.activation(cen[:, t, :], dp[:], IDENTITY, bias=neg_delta[:, t : t + 1])
             centred.append(cen)
 
         qm_bf = sb.tile([P, D, PACK], BF16, name="qm_bf", align_bytes=64)
         nc.vector.tensor_copy(
-            qm_bf[:].rearrange("p (c i) t -> p c t i", i=2), qm_raw[:].rearrange("p t (c i) -> p c t i", i=2)
+            qm_bf[:].rearrange("p (c i) t -> p c t i", i=4), qm_raw[:].rearrange("p t (c i) -> p c t i", i=4)
         )
         qm_codes = sb.tile([P, D], U32, name="qm_codes", align_bytes=64)
         qm_sc = sb.tile([P, D], U8, name="qm_sc", align_bytes=64)
         nc.vector.quantize_mx(qm_codes[:].bitcast(FP8X4), qm_sc[:], qm_bf[:].rearrange("p d t -> p (d t)"))
 
-        dk = [sb.tile([P, N], F32, name=f"dk{c}") for c in range(2)]
-        for h in range(2):
-            ds_bf = sb.tile([P, HALF, PACK], BF16, name=f"ds_bf{h}", align_bytes=64)
+        def quantize_ds(h):
+            ds_bf = sb.tile([P, HALF, PACK], BF16, name="ds_bf", align_bytes=64)
             nc.vector.tensor_tensor(
-                ds_bf[:].rearrange("p (c i) t -> p c t i", i=2),
-                centred[h][:].rearrange("p t (c i) -> p c t i", i=2),
-                p_raw[h][:].rearrange("p t (c i) -> p c t i", i=2),
+                ds_bf[:].rearrange("p (c i) t -> p c t i", i=4),
+                centred[h][:].rearrange("p t (c i) -> p c t i", i=4),
+                p_raw[h][:].rearrange("p t (c i) -> p c t i", i=4),
                 MULT,
             )
             ds_codes = sb.tile([P, HALF], U32, name=f"ds_codes{h}", align_bytes=64)
             ds_sc = sb.tile([P, HALF], U8, name=f"ds_sc{h}", align_bytes=64)
             nc.vector.quantize_mx(ds_codes[:].bitcast(FP8X4), ds_sc[:], ds_bf[:].rearrange("p n t -> p (n t)"))
-            for c in range(2):
-                acc = ps.tile([P, HALF], F32, name=f"dk_acc{h}{c}")
-                nc.tensor.matmul_mx(
-                    acc[:],
-                    lhsT=qm_codes[:, c * P : (c + 1) * P].bitcast(FP8X4),
-                    lhsT_scale=qm_sc[:, c * P : (c + 1) * P],
-                    rhs=ds_codes[:].bitcast(FP8X4),
-                    rhs_scale=ds_sc[:],
-                    start=True,
-                    stop=True,
-                )
-                nc.scalar.copy(dk[c][:, h * HALF : (h + 1) * HALF], acc[:])
+            return ds_codes, ds_sc
+
+        def dk_product(ds, h, c):
+            acc = ps.tile([P, HALF], F32, name=f"bank{2 * h + c}")
+            nc.tensor.matmul_mx(
+                acc[:],
+                lhsT=qm_codes[:, c * P : (c + 1) * P].bitcast(FP8X4),
+                lhsT_scale=qm_sc[:, c * P : (c + 1) * P],
+                rhs=ds[0][:].bitcast(FP8X4),
+                rhs_scale=ds[1][:],
+                start=True,
+                stop=True,
+            )
+            return acc
+
+        dk_second = sb.tile([P, N], F32, name="dk_second")
+        ds = quantize_ds(0)
+        acc_first, acc_second = dk_product(ds, 0, 0), dk_product(ds, 0, 1)
+        nc.scalar.copy(dk_second[:, 0:HALF], acc_second[:])
+        ds = quantize_ds(1)
+        dk_first = [sb.tile([P, HALF], F32, name=f"centred{1 - h}") for h in range(2)]
+        nc.scalar.copy(dk_first[0][:], acc_first[:])
+        nc.scalar.copy(dk_first[1][:], dk_product(ds, 1, 0)[:])
+        nc.scalar.copy(dk_second[:, HALF:N], dk_product(ds, 1, 1)[:])
 
         for h in range(2):
-            nc.vector.tensor_copy(windows[0][:].indirect(list_half(h)), dk[0][:, h * HALF : (h + 1) * HALF])
+            nc.vector.tensor_copy(windows[0][:].indirect(list_half(h)), dk_first[h][:])
         nc.sync.dma_start(out[0:P, :], windows[0][:])
-        nc.vector.tensor_copy(windows[1][:].indirect(offsets[:]), dk[1][:])
+        nc.vector.tensor_copy(windows[1][:].indirect(offsets[:]), dk_second[:])
         nc.sync.dma_start(out[P : 2 * P, :], windows[1][:])

@@ -46,8 +46,8 @@ def tile_attend_bwd_kernel(tc, doT, v_words, v_scales, p, delta, qm, offs, out):
         nc.sync.dma_start(offsets[:], offs)
         nc.sync.dma_start(delta_raw[:], delta[0].rearrange("(p t) o -> p (t o)", t=PACK))
         scale_rows = v_scales[0].bitcast(I32)
-        for quad in range(4):
-            nc.sync.dma_start(pool_scales[32 * quad : 32 * quad + 4, :], scale_rows[4 * quad : 4 * quad + 4, :])
+        for r in range(4):
+            nc.sync.dma_start(pool_scales[r:P:32, :], scale_rows[r:16:4, :])
         nc.sync.dma_start(pool_words[:], v_words[0].rearrange("p n r -> p (n r)").bitcast(I32))
         nc.sync.dma_start(qm_raw[:], qm[0].rearrange("(p t) d -> p t d", t=PACK))
         p_rows = p[0].rearrange("(p t) n -> p t n", t=PACK)
@@ -102,16 +102,21 @@ def tile_attend_bwd_kernel(tc, doT, v_words, v_scales, p, delta, qm, offs, out):
         nc.vector.quantize_mx(qm_codes[:].bitcast(FP8X4), qm_sc[:], qm_bf[:].rearrange("p d t -> p (d t)"))
 
         def quantize_ds(h):
-            ds_bf = sb.tile([P, HALF, PACK], BF16, name="ds_bf", align_bytes=64)
-            nc.vector.tensor_tensor(
-                ds_bf[:].rearrange("p (c i) t -> p c t i", i=4),
-                centred[h][:].rearrange("p t (c i) -> p c t i", i=4),
-                p_raw[h][:].rearrange("p t (c i) -> p c t i", i=4),
-                MULT,
-            )
             ds_codes = sb.tile([P, HALF], U32, name=f"ds_codes{h}", align_bytes=64)
             ds_sc = sb.tile([P, HALF], U8, name=f"ds_sc{h}", align_bytes=64)
-            nc.vector.quantize_mx(ds_codes[:].bitcast(FP8X4), ds_sc[:], ds_bf[:].rearrange("p n t -> p (n t)"))
+            pieces = [slice(s * P, (s + 1) * P) for s in range(2)]
+            ds_bf = [sb.tile([P, P, PACK], BF16, name=f"ds_bf{s}", align_bytes=64) for s in range(2)]
+            for s in range(2):
+                nc.vector.tensor_tensor(
+                    ds_bf[s][:].rearrange("p (c i) t -> p c t i", i=4),
+                    centred[h][:, :, pieces[s]].rearrange("p t (c i) -> p c t i", i=4),
+                    p_raw[h][:, :, pieces[s]].rearrange("p t (c i) -> p c t i", i=4),
+                    MULT,
+                )
+            for s in range(2):
+                nc.vector.quantize_mx(
+                    ds_codes[:, pieces[s]].bitcast(FP8X4), ds_sc[:, pieces[s]], ds_bf[s][:].rearrange("p n t -> p (n t)")
+                )
             return ds_codes, ds_sc
 
         def dk_product(ds, h, c):

@@ -18,7 +18,18 @@ MULT = mybir.AluOpType.mult
 P = 128
 PACK = 4
 HALF = N // 2
+PIECE = HALF // 2
 LIST_COLS = N // 16
+SCALE_WORDS = T // 4
+RUN = 4
+
+
+def in_runs(rows):
+    return rows.rearrange("p t (c i) -> p c t i", i=RUN)
+
+
+def interleaved(words):
+    return words.rearrange("p (c i) t -> p c t i", i=RUN)
 
 
 def tile_attend_bwd_kernel(tc, doT, v_words, v_scales, p, delta, qm, offs, out):
@@ -28,11 +39,13 @@ def tile_attend_bwd_kernel(tc, doT, v_words, v_scales, p, delta, qm, offs, out):
         ps = ctx.enter_context(tc.psum_pool(name="ps", bufs=1))
 
         offsets = sb.tile([P, LIST_COLS], U16, name="offsets")
-        pool_scales = sb.tile([P, T // 4], I32, name="pool_scales")
+        pool_scales = sb.tile([P, SCALE_WORDS], I32, name="pool_scales")
         pool_words = sb.tile([P, T], I32, name="pool_words")
         do_raw = sb.tile([P, PACK, NQ], F32, name="do_raw")
         qm_raw = sb.tile([P, PACK, D], F32, name="qm_raw")
-        p_raw = [sb.tile([P, PACK, HALF], F32, name=f"p_raw{h}") for h in range(2)]
+        p_head = sb.tile([P, PACK, HALF], F32, name="p_head")
+        p_tail = [sb.tile([P, PACK, PIECE], F32, name=f"p_tail{s}") for s in range(2)]
+        p_piece = [[p_head[:, :, s * PIECE : (s + 1) * PIECE] for s in range(2)], [p_tail[s][:] for s in range(2)]]
         delta_raw = sb.tile([P, PACK], F32, name="delta_raw")
         neg_delta = sb.tile([P, PACK], F32, name="neg_delta")
         windows = [sb.tile([P, T], F32, name=f"window{c}") for c in range(2)]
@@ -40,8 +53,9 @@ def tile_attend_bwd_kernel(tc, doT, v_words, v_scales, p, delta, qm, offs, out):
         def list_half(h):
             return offsets[:, h * (LIST_COLS // 2) : (h + 1) * (LIST_COLS // 2)]
 
-        nc.vector.memset(pool_scales[:, 0 : T // 8], 0)
-        nc.gpsimd.memset(pool_scales[:, T // 8 : T // 4], 0)
+        nc.vector.memset(pool_scales[:, 0 : SCALE_WORDS // 2], 0)
+        nc.gpsimd.memset(pool_scales[:, SCALE_WORDS // 2 : SCALE_WORDS], 0)
+
         nc.sync.dma_start(do_raw[:], doT[0].rearrange("(p j) q -> p j q", j=PACK))
         nc.sync.dma_start(offsets[:], offs)
         nc.sync.dma_start(delta_raw[:], delta[0].rearrange("(p t) o -> p (t o)", t=PACK))
@@ -51,99 +65,96 @@ def tile_attend_bwd_kernel(tc, doT, v_words, v_scales, p, delta, qm, offs, out):
         nc.sync.dma_start(pool_words[:], v_words[0].rearrange("p n r -> p (n r)").bitcast(I32))
         nc.sync.dma_start(qm_raw[:], qm[0].rearrange("(p t) d -> p t d", t=PACK))
         p_rows = p[0].rearrange("(p t) n -> p t n", t=PACK)
-        for h in range(2):
-            nc.sync.dma_start(p_raw[h][:], p_rows[:, :, h * HALF : (h + 1) * HALF])
+        nc.sync.dma_start(p_head[:], p_rows[:, :, 0:HALF])
+        for s in range(2):
+            nc.sync.dma_start(p_tail[s][:], p_rows[:, :, HALF + s * PIECE : HALF + (s + 1) * PIECE])
 
         nc.vector.memset(windows[0][:].bitcast(I32), 0)
         nc.gpsimd.memset(windows[1][:].bitcast(I32), 0)
         nc.scalar.activation(neg_delta[:], delta_raw[:], IDENTITY, scale=-1.0)
 
-        do_codes, do_sc = [], []
-        do_src = do_raw[:].rearrange("p j (m u e) -> p u m j e", u=2, e=2)
+        do_codes, do_scales = [], []
+        do_by_u = do_raw[:].rearrange("p j (m u w) -> p u m j w", u=2, w=2)
         do_bf = [sb.tile([P, 2, P, PACK], BF16, name=f"do_bf{u}", align_bytes=64) for u in range(2)]
-        nc.vector.tensor_copy(do_bf[0][:].rearrange("p e m j -> p m j e"), do_src[:, 0])
-        nc.scalar.copy(do_bf[1][:].rearrange("p e m j -> p m j e"), do_src[:, 1])
+        nc.vector.tensor_copy(do_bf[0][:].rearrange("p w m j -> p m j w"), do_by_u[:, 0])
+        nc.scalar.copy(do_bf[1][:].rearrange("p w m j -> p m j w"), do_by_u[:, 1])
         for u in range(2):
             codes = sb.tile([P, 2 * P], U32, name=f"do_codes{u}", align_bytes=64)
-            sc = sb.tile([P, 2 * P], U8, name=f"do_sc{u}", align_bytes=64)
-            nc.vector.quantize_mx(codes[:].bitcast(FP8X4), sc[:], do_bf[u][:].rearrange("p e m j -> p (e m j)"))
+            scales = sb.tile([P, 2 * P], U8, name=f"do_scales{u}", align_bytes=64)
+            nc.vector.quantize_mx(codes[:].bitcast(FP8X4), scales[:], do_bf[u][:].rearrange("p w m j -> p (w m j)"))
             do_codes.append(codes)
-            do_sc.append(sc)
+            do_scales.append(scales)
 
-        v_sc = sb.tile([P, N], U8, name="v_sc", align_bytes=64)
-        nc.vector.tensor_copy(v_sc[:], pool_scales[:].bitcast(U8).indirect(offsets[:]))
+        v_sel_scales = sb.tile([P, N], U8, name="v_sel_scales", align_bytes=64)
+        nc.vector.tensor_copy(v_sel_scales[:], pool_scales[:].bitcast(U8).indirect(offsets[:]))
 
         centred = []
         for h in range(2):
-            v_codes = sb.tile([P, HALF], U32, name=f"v_codes{h}", align_bytes=64)
-            nc.vector.tensor_copy(v_codes[:], pool_words[:].bitcast(U32).indirect(list_half(h)))
-            cen = sb.tile([P, PACK, HALF], F32, name=f"centred{h}")
+            v_sel_words = sb.tile([P, HALF], U32, name=f"v_sel_words{h}", align_bytes=64)
+            nc.vector.tensor_copy(v_sel_words[:], pool_words[:].bitcast(U32).indirect(list_half(h)))
+            dp_less_delta = sb.tile([P, PACK, HALF], F32, name=f"centred{h}")
             for t in range(PACK):
-                u, e = divmod(t, 2)
+                u, w = divmod(t, 2)
                 dp = ps.tile([P, HALF], F32, name=f"bank{PACK * h + t}")
                 nc.tensor.matmul_mx(
                     dp[:],
-                    lhsT=do_codes[u][:, e * P : (e + 1) * P].bitcast(FP8X4),
-                    lhsT_scale=do_sc[u][:, e * P : (e + 1) * P],
-                    rhs=v_codes[:].bitcast(FP8X4),
-                    rhs_scale=v_sc[:, h * HALF : (h + 1) * HALF],
+                    lhsT=do_codes[u][:, w * P : (w + 1) * P].bitcast(FP8X4),
+                    lhsT_scale=do_scales[u][:, w * P : (w + 1) * P],
+                    rhs=v_sel_words[:].bitcast(FP8X4),
+                    rhs_scale=v_sel_scales[:, h * HALF : (h + 1) * HALF],
                     start=True,
                     stop=True,
                 )
-                nc.scalar.activation(cen[:, t, :], dp[:], IDENTITY, bias=neg_delta[:, t : t + 1])
-            centred.append(cen)
+                nc.scalar.activation(dp_less_delta[:, t, :], dp[:], IDENTITY, bias=neg_delta[:, t : t + 1])
+            centred.append(dp_less_delta)
 
         qm_bf = sb.tile([P, D, PACK], BF16, name="qm_bf", align_bytes=64)
-        nc.vector.tensor_copy(
-            qm_bf[:].rearrange("p (c i) t -> p c t i", i=4), qm_raw[:].rearrange("p t (c i) -> p c t i", i=4)
-        )
+        nc.vector.tensor_copy(interleaved(qm_bf[:]), in_runs(qm_raw[:]))
         qm_codes = sb.tile([P, D], U32, name="qm_codes", align_bytes=64)
-        qm_sc = sb.tile([P, D], U8, name="qm_sc", align_bytes=64)
-        nc.vector.quantize_mx(qm_codes[:].bitcast(FP8X4), qm_sc[:], qm_bf[:].rearrange("p d t -> p (d t)"))
+        qm_scales = sb.tile([P, D], U8, name="qm_scales", align_bytes=64)
+        nc.vector.quantize_mx(qm_codes[:].bitcast(FP8X4), qm_scales[:], qm_bf[:].rearrange("p d t -> p (d t)"))
 
         def quantize_ds(h):
-            ds_codes = sb.tile([P, HALF], U32, name=f"ds_codes{h}", align_bytes=64)
-            ds_sc = sb.tile([P, HALF], U8, name=f"ds_sc{h}", align_bytes=64)
-            pieces = [slice(s * P, (s + 1) * P) for s in range(2)]
-            ds_bf = [sb.tile([P, P, PACK], BF16, name=f"ds_bf{s}", align_bytes=64) for s in range(2)]
+            codes = sb.tile([P, HALF], U32, name=f"ds_codes{h}", align_bytes=64)
+            scales = sb.tile([P, HALF], U8, name=f"ds_scales{h}", align_bytes=64)
+            pieces = [slice(s * PIECE, (s + 1) * PIECE) for s in range(2)]
+            ds_bf = [sb.tile([P, PIECE, PACK], BF16, name=f"ds_bf{s}", align_bytes=64) for s in range(2)]
             for s in range(2):
                 nc.vector.tensor_tensor(
-                    ds_bf[s][:].rearrange("p (c i) t -> p c t i", i=4),
-                    centred[h][:, :, pieces[s]].rearrange("p t (c i) -> p c t i", i=4),
-                    p_raw[h][:, :, pieces[s]].rearrange("p t (c i) -> p c t i", i=4),
-                    MULT,
+                    interleaved(ds_bf[s][:]), in_runs(centred[h][:, :, pieces[s]]), in_runs(p_piece[h][s]), MULT
                 )
             for s in range(2):
                 nc.vector.quantize_mx(
-                    ds_codes[:, pieces[s]].bitcast(FP8X4), ds_sc[:, pieces[s]], ds_bf[s][:].rearrange("p n t -> p (n t)")
+                    codes[:, pieces[s]].bitcast(FP8X4), scales[:, pieces[s]], ds_bf[s][:].rearrange("p n t -> p (n t)")
                 )
-            return ds_codes, ds_sc
+            return codes, scales
 
         def dk_product(ds, h, c):
+            ds_codes, ds_scales = ds
             acc = ps.tile([P, HALF], F32, name=f"bank{2 * h + c}")
             nc.tensor.matmul_mx(
                 acc[:],
                 lhsT=qm_codes[:, c * P : (c + 1) * P].bitcast(FP8X4),
-                lhsT_scale=qm_sc[:, c * P : (c + 1) * P],
-                rhs=ds[0][:].bitcast(FP8X4),
-                rhs_scale=ds[1][:],
+                lhsT_scale=qm_scales[:, c * P : (c + 1) * P],
+                rhs=ds_codes[:].bitcast(FP8X4),
+                rhs_scale=ds_scales[:],
                 start=True,
                 stop=True,
             )
             return acc
 
-        dk_second = sb.tile([P, N], F32, name="dk_second")
+        dk_high = sb.tile([P, N], F32, name="dk_high")
         ds = quantize_ds(0)
-        acc_first, acc_second = dk_product(ds, 0, 0), dk_product(ds, 0, 1)
-        nc.scalar.copy(dk_second[:, 0:HALF], acc_second[:])
+        acc_low, acc_high = dk_product(ds, 0, 0), dk_product(ds, 0, 1)
+        nc.scalar.copy(dk_high[:, 0:HALF], acc_high[:])
         ds = quantize_ds(1)
-        dk_first = [sb.tile([P, HALF], F32, name=f"centred{1 - h}") for h in range(2)]
-        nc.scalar.copy(dk_first[0][:], acc_first[:])
-        nc.scalar.copy(dk_first[1][:], dk_product(ds, 1, 0)[:])
-        nc.scalar.copy(dk_second[:, HALF:N], dk_product(ds, 1, 1)[:])
+        dk_low = [sb.tile([P, HALF], F32, name=("p_tail0", "centred0")[h]) for h in range(2)]
+        nc.scalar.copy(dk_low[0][:], acc_low[:])
+        nc.scalar.copy(dk_low[1][:], dk_product(ds, 1, 0)[:])
+        nc.scalar.copy(dk_high[:, HALF:N], dk_product(ds, 1, 1)[:])
 
         for h in range(2):
-            nc.vector.tensor_copy(windows[0][:].indirect(list_half(h)), dk_first[h][:])
+            nc.vector.tensor_copy(windows[0][:].indirect(list_half(h)), dk_low[h][:])
         nc.sync.dma_start(out[0:P, :], windows[0][:])
-        nc.vector.tensor_copy(windows[1][:].indirect(offsets[:]), dk_second[:])
+        nc.vector.tensor_copy(windows[1][:].indirect(offsets[:]), dk_high[:])
         nc.sync.dma_start(out[P : 2 * P, :], windows[1][:])

@@ -12,8 +12,8 @@ U32 = mybir.dt.uint32
 U16 = mybir.dt.uint16
 U8 = mybir.dt.uint8
 FP8X4 = mybir.dt.float8_e4m3fn_x4
-IDENTITY = mybir.ActivationFunctionType.Identity
 MULT = mybir.AluOpType.mult
+SUBTRACT = mybir.AluOpType.subtract
 
 P = 128
 PACK = 4
@@ -39,43 +39,46 @@ def tile_attend_bwd_kernel(tc, doT, v_words, v_scales, p, delta, qm, offs, out):
         ps = ctx.enter_context(tc.psum_pool(name="ps", bufs=1))
 
         offsets = sb.tile([P, LIST_COLS], U16, name="offsets")
-        pool_scales = sb.tile([P, SCALE_WORDS], I32, name="pool_scales")
+        pool_scales = sb.tile([P, SCALE_WORDS], I32, name="pool_scales", align_bytes=64)
         pool_words = sb.tile([P, T], I32, name="pool_words")
         do_raw = sb.tile([P, PACK, NQ], F32, name="do_raw")
         qm_raw = sb.tile([P, PACK, D], F32, name="qm_raw")
-        p_head = sb.tile([P, PACK, HALF], F32, name="p_head")
-        p_tail = [sb.tile([P, PACK, PIECE], F32, name=f"p_tail{s}") for s in range(2)]
-        p_piece = [[p_head[:, :, s * PIECE : (s + 1) * PIECE] for s in range(2)], [p_tail[s][:] for s in range(2)]]
+        p_half = [sb.tile([P, PACK, HALF], F32, name=f"p_half{h}") for h in range(2)]
         delta_raw = sb.tile([P, PACK], F32, name="delta_raw")
-        neg_delta = sb.tile([P, PACK], F32, name="neg_delta")
         windows = [sb.tile([P, T], F32, name=f"window{c}") for c in range(2)]
 
         def list_half(h):
             return offsets[:, h * (LIST_COLS // 2) : (h + 1) * (LIST_COLS // 2)]
 
-        nc.vector.memset(pool_scales[:, 0 : SCALE_WORDS // 2], 0)
-        nc.gpsimd.memset(pool_scales[:, SCALE_WORDS // 2 : SCALE_WORDS], 0)
+        nc.gpsimd.memset(pool_scales[:], 0)
 
-        nc.sync.dma_start(do_raw[:], doT[0].rearrange("(p j) q -> p j q", j=PACK))
+        do_rows = doT[0].rearrange("(p j) q -> p j q", j=PACK)
+        nc.sync.dma_start(do_raw[:, 0:2, :], do_rows[:, 0:2, :])
         nc.sync.dma_start(offsets[:], offs)
-        nc.sync.dma_start(delta_raw[:], delta[0].rearrange("(p t) o -> p (t o)", t=PACK))
         scale_rows = v_scales[0].bitcast(I32)
         for r in range(4):
             nc.sync.dma_start(pool_scales[r:P:32, :], scale_rows[r:16:4, :])
+        nc.sync.dma_start(do_raw[:, 2:4, :], do_rows[:, 2:4, :])
         nc.sync.dma_start(pool_words[:], v_words[0].rearrange("p n r -> p (n r)").bitcast(I32))
-        nc.sync.dma_start(qm_raw[:], qm[0].rearrange("(p t) d -> p t d", t=PACK))
+        nc.sync.dma_start(delta_raw[:], delta[0].rearrange("(p t) o -> p (t o)", t=PACK))
         p_rows = p[0].rearrange("(p t) n -> p t n", t=PACK)
-        nc.sync.dma_start(p_head[:], p_rows[:, :, 0:HALF])
-        for s in range(2):
-            nc.sync.dma_start(p_tail[s][:], p_rows[:, :, HALF + s * PIECE : HALF + (s + 1) * PIECE])
+        nc.sync.dma_start(p_half[0][:], p_rows[:, :, 0:HALF])
+        nc.sync.dma_start(qm_raw[:], qm[0].rearrange("(p t) d -> p t d", t=PACK))
+        for u in range(2):
+            nc.sync.dma_start(p_half[1][:, 2 * u : 2 * u + 2, :], p_rows[:, 2 * u : 2 * u + 2, HALF:N])
 
+        warm = sb.tile([P, 2], F32, name="warm")
+        nc.vector.memset(warm[:, 0:1], 0.0)
+        nc.scalar.copy(warm[:, 1:2], warm[:, 0:1])
         nc.vector.memset(windows[0][:].bitcast(I32), 0)
         nc.gpsimd.memset(windows[1][:].bitcast(I32), 0)
-        nc.scalar.activation(neg_delta[:], delta_raw[:], IDENTITY, scale=-1.0)
+
+        v_sel_scales = sb.tile([P, N], U8, name="v_sel_scales", align_bytes=64)
+        nc.vector.tensor_copy(v_sel_scales[:], pool_scales[:].bitcast(U8).indirect(offsets[:]))
 
         do_codes, do_scales = [], []
         do_by_u = do_raw[:].rearrange("p j (m u w) -> p u m j w", u=2, w=2)
-        do_bf = [sb.tile([P, 2, P, PACK], BF16, name=f"do_bf{u}", align_bytes=64) for u in range(2)]
+        do_bf = [sb.tile([P, 2, P, PACK], BF16, name=("pool_scales", "do_bf1")[u], align_bytes=64) for u in range(2)]
         nc.vector.tensor_copy(do_bf[0][:].rearrange("p w m j -> p m j w"), do_by_u[:, 0])
         nc.scalar.copy(do_bf[1][:].rearrange("p w m j -> p m j w"), do_by_u[:, 1])
         for u in range(2):
@@ -85,19 +88,16 @@ def tile_attend_bwd_kernel(tc, doT, v_words, v_scales, p, delta, qm, offs, out):
             do_codes.append(codes)
             do_scales.append(scales)
 
-        v_sel_scales = sb.tile([P, N], U8, name="v_sel_scales", align_bytes=64)
-        nc.vector.tensor_copy(v_sel_scales[:], pool_scales[:].bitcast(U8).indirect(offsets[:]))
-
-        centred = []
+        dp = []
         for h in range(2):
-            v_sel_words = sb.tile([P, HALF], U32, name=f"v_sel_words{h}", align_bytes=64)
+            v_sel_words = sb.tile([P, HALF], U32, name=("pool_scales", "do_bf1")[h], align_bytes=64)
             nc.vector.tensor_copy(v_sel_words[:], pool_words[:].bitcast(U32).indirect(list_half(h)))
-            dp_less_delta = sb.tile([P, PACK, HALF], F32, name=f"centred{h}")
+            banks = []
             for t in range(PACK):
                 u, w = divmod(t, 2)
-                dp = ps.tile([P, HALF], F32, name=f"bank{PACK * h + t}")
+                bank = ps.tile([P, HALF], F32, name=f"bank{PACK * h + t}")
                 nc.tensor.matmul_mx(
-                    dp[:],
+                    bank[:],
                     lhsT=do_codes[u][:, w * P : (w + 1) * P].bitcast(FP8X4),
                     lhsT_scale=do_scales[u][:, w * P : (w + 1) * P],
                     rhs=v_sel_words[:].bitcast(FP8X4),
@@ -105,56 +105,73 @@ def tile_attend_bwd_kernel(tc, doT, v_words, v_scales, p, delta, qm, offs, out):
                     start=True,
                     stop=True,
                 )
-                nc.scalar.activation(dp_less_delta[:, t, :], dp[:], IDENTITY, bias=neg_delta[:, t : t + 1])
-            centred.append(dp_less_delta)
+                banks.append(bank)
+            dp.append(banks)
 
-        qm_bf = sb.tile([P, D, PACK], BF16, name="qm_bf", align_bytes=64)
-        nc.vector.tensor_copy(interleaved(qm_bf[:]), in_runs(qm_raw[:]))
-        qm_codes = sb.tile([P, D], U32, name="qm_codes", align_bytes=64)
-        qm_scales = sb.tile([P, D], U8, name="qm_scales", align_bytes=64)
-        nc.vector.quantize_mx(qm_codes[:].bitcast(FP8X4), qm_scales[:], qm_bf[:].rearrange("p d t -> p (d t)"))
+        ds_rows = [sb.tile([P, PACK, HALF], BF16, name=f"ds_rows{h}") for h in range(2)]
 
-        def quantize_ds(h):
-            codes = sb.tile([P, HALF], U32, name=f"ds_codes{h}", align_bytes=64)
-            scales = sb.tile([P, HALF], U8, name=f"ds_scales{h}", align_bytes=64)
-            pieces = [slice(s * PIECE, (s + 1) * PIECE) for s in range(2)]
-            ds_bf = [sb.tile([P, PIECE, PACK], BF16, name=f"ds_bf{s}", align_bytes=64) for s in range(2)]
-            for s in range(2):
-                nc.vector.tensor_tensor(
-                    interleaved(ds_bf[s][:]), in_runs(centred[h][:, :, pieces[s]]), in_runs(p_piece[h][s]), MULT
-                )
-            for s in range(2):
-                nc.vector.quantize_mx(
-                    codes[:, pieces[s]].bitcast(FP8X4), scales[:, pieces[s]], ds_bf[s][:].rearrange("p n t -> p (n t)")
-                )
-            return codes, scales
+        def ds_row(h, t):
+            nc.vector.scalar_tensor_tensor(
+                ds_rows[h][:, t, :], dp[h][t][:], delta_raw[:, t : t + 1], p_half[h][:, t, :], SUBTRACT, MULT
+            )
 
-        def dk_product(ds, h, c):
-            ds_codes, ds_scales = ds
-            acc = ps.tile([P, HALF], F32, name=f"bank{2 * h + c}")
+        ds_codes = sb.tile([P, N], U32, name="ds_codes", align_bytes=64)
+        ds_scales = sb.tile([P, N], U8, name="ds_scales", align_bytes=64)
+
+        def quantize(codes, scales, words):
+            nc.vector.quantize_mx(codes.bitcast(FP8X4), scales, words.rearrange("p n t -> p (n t)"))
+
+        def quantize_ds(first, words, width):
+            quantize(ds_codes[:, first : first + width], ds_scales[:, first : first + width], words[:])
+
+        qm_bf = [sb.tile([P, P, PACK], BF16, name=f"qm_bf{c}", align_bytes=64) for c in range(2)]
+        qm_codes = [sb.tile([P, P], U32, name=f"qm_codes{c}", align_bytes=64) for c in range(2)]
+        qm_scales = [sb.tile([P, P], U8, name=f"qm_scales{c}", align_bytes=64) for c in range(2)]
+
+        def interleave_qm(c):
+            nc.scalar.copy(interleaved(qm_bf[c][:]), in_runs(qm_raw[:, :, c * P : (c + 1) * P]))
+
+        def dk_product(c, first, width, bank):
+            acc = ps.tile([P, width], F32, name=f"bank{bank}")
             nc.tensor.matmul_mx(
                 acc[:],
-                lhsT=qm_codes[:, c * P : (c + 1) * P].bitcast(FP8X4),
-                lhsT_scale=qm_scales[:, c * P : (c + 1) * P],
-                rhs=ds_codes[:].bitcast(FP8X4),
-                rhs_scale=ds_scales[:],
+                lhsT=qm_codes[c][:].bitcast(FP8X4),
+                lhsT_scale=qm_scales[c][:],
+                rhs=ds_codes[:, first : first + width].bitcast(FP8X4),
+                rhs_scale=ds_scales[:, first : first + width],
                 start=True,
                 stop=True,
             )
             return acc
 
-        dk_high = sb.tile([P, N], F32, name="dk_high")
-        ds = quantize_ds(0)
-        acc_low, acc_high = dk_product(ds, 0, 0), dk_product(ds, 0, 1)
-        nc.scalar.copy(dk_high[:, 0:HALF], acc_high[:])
-        ds = quantize_ds(1)
-        dk_low = [sb.tile([P, HALF], F32, name=("p_tail0", "centred0")[h]) for h in range(2)]
-        nc.scalar.copy(dk_low[0][:], acc_low[:])
-        nc.scalar.copy(dk_low[1][:], dk_product(ds, 1, 0)[:])
-        nc.scalar.copy(dk_high[:, HALF:N], dk_product(ds, 1, 1)[:])
+        ds_first = sb.tile([P, HALF, PACK], BF16, name="ds_first", align_bytes=64)
+        ds_third = sb.tile([P, PIECE, PACK], BF16, name="ds_third", align_bytes=64)
+        ds_last = sb.tile([P, PIECE, PACK], BF16, name="ds_last", align_bytes=64)
+        for t in range(PACK):
+            ds_row(0, t)
+        interleave_qm(0)
+        nc.scalar.copy(interleaved(ds_first[:]), in_runs(ds_rows[0][:]))
+        interleave_qm(1)
+        ds_row(1, 0)
+        ds_row(1, 1)
+        quantize(qm_codes[0][:], qm_scales[0][:], qm_bf[0][:])
+        ds_row(1, 2)
+        quantize_ds(0, ds_first, HALF)
+        ds_row(1, 3)
+        nc.scalar.copy(interleaved(ds_third[:]), in_runs(ds_rows[1][:, :, 0:PIECE]))
+        nc.vector.tensor_copy(interleaved(ds_last[:]), in_runs(ds_rows[1][:, :, PIECE:HALF]))
+        acc_low = dk_product(0, 0, HALF, 0)
+        quantize_ds(HALF, ds_third, PIECE)
+        quantize_ds(HALF + PIECE, ds_last, PIECE)
 
-        for h in range(2):
-            nc.vector.tensor_copy(windows[0][:].indirect(list_half(h)), dk_low[h][:])
+        dk_low = [sb.tile([P, HALF], F32, name=f"dk_low{h}") for h in range(2)]
+        dk_high = sb.tile([P, N], F32, name="dk_high")
+        nc.scalar.copy(dk_low[0][:], acc_low[:])
+        quantize(qm_codes[1][:], qm_scales[1][:], qm_bf[1][:])
+        nc.scalar.copy(dk_low[1][:], dk_product(0, HALF, HALF, 1)[:])
+        nc.vector.tensor_copy(windows[0][:].indirect(list_half(0)), dk_low[0][:])
+        nc.scalar.copy(dk_high[:], dk_product(1, 0, N, 2)[:])
+        nc.vector.tensor_copy(windows[0][:].indirect(list_half(1)), dk_low[1][:])
         nc.sync.dma_start(out[0:P, :], windows[0][:])
         nc.vector.tensor_copy(windows[1][:].indirect(offsets[:]), dk_high[:])
         nc.sync.dma_start(out[P : 2 * P, :], windows[1][:])

@@ -88,6 +88,18 @@ def tile_attend_bwd_kernel(tc, doT, v_words, v_scales, p, delta, qm, offs, out):
             do_codes.append(codes)
             do_scales.append(scales)
 
+        warm_bank = ps.tile([P, HALF], F32, name="bank7")
+        for w in range(3):
+            nc.tensor.matmul_mx(
+                warm_bank[:],
+                lhsT=do_codes[1][:, 0:P].bitcast(FP8X4),
+                lhsT_scale=do_scales[1][:, 0:P],
+                rhs=do_codes[1][:].bitcast(FP8X4),
+                rhs_scale=do_scales[1][:],
+                start=True,
+                stop=True,
+            )
+
         dp = []
         for h in range(2):
             v_sel_words = sb.tile([P, HALF], U32, name=("pool_scales", "do_bf1")[h], align_bytes=64)

@@ -14,6 +14,7 @@ U8 = mybir.dt.uint8
 FP8X4 = mybir.dt.float8_e4m3fn_x4
 MULT = mybir.AluOpType.mult
 SUBTRACT = mybir.AluOpType.subtract
+ADD = mybir.AluOpType.add
 
 P = 128
 PACK = 4
@@ -72,6 +73,8 @@ def tile_attend_bwd_kernel(tc, doT, v_words, v_scales, p, delta, qm, offs, out):
         nc.scalar.copy(warm[:, 1:2], warm[:, 0:1])
         nc.vector.memset(windows[0][:].bitcast(I32), 0)
         nc.gpsimd.memset(windows[1][:].bitcast(I32), 0)
+        zeros = sb.tile([P, PIECE], F32, name="zeros")
+        nc.gpsimd.memset(zeros[:], 0.0)
 
         v_sel_scales = sb.tile([P, N], U8, name="v_sel_scales", align_bytes=64)
         nc.vector.tensor_copy(v_sel_scales[:], pool_scales[:].bitcast(U8).indirect(offsets[:]))
@@ -88,44 +91,31 @@ def tile_attend_bwd_kernel(tc, doT, v_words, v_scales, p, delta, qm, offs, out):
             do_codes.append(codes)
             do_scales.append(scales)
 
-        warm_bank = ps.tile([P, HALF], F32, name="bank7")
-        for w in range(3):
-            nc.tensor.matmul_mx(
-                warm_bank[:],
-                lhsT=do_codes[1][:, 0:P].bitcast(FP8X4),
-                lhsT_scale=do_scales[1][:, 0:P],
-                rhs=do_codes[1][:].bitcast(FP8X4),
-                rhs_scale=do_scales[1][:],
-                start=True,
-                stop=True,
-            )
-
-        dp = []
-        for h in range(2):
-            v_sel_words = sb.tile([P, HALF], U32, name=("pool_scales", "do_bf1")[h], align_bytes=64)
-            nc.vector.tensor_copy(v_sel_words[:], pool_words[:].bitcast(U32).indirect(list_half(h)))
+        def dp_products(words, first, width, bank0):
             banks = []
             for t in range(PACK):
                 u, w = divmod(t, 2)
-                bank = ps.tile([P, HALF], F32, name=f"bank{PACK * h + t}")
+                bank = ps.tile([P, width], F32, name=f"bank{bank0 + t}")
                 nc.tensor.matmul_mx(
                     bank[:],
                     lhsT=do_codes[u][:, w * P : (w + 1) * P].bitcast(FP8X4),
                     lhsT_scale=do_scales[u][:, w * P : (w + 1) * P],
-                    rhs=v_sel_words[:].bitcast(FP8X4),
-                    rhs_scale=v_sel_scales[:, h * HALF : (h + 1) * HALF],
+                    rhs=words.bitcast(FP8X4),
+                    rhs_scale=v_sel_scales[:, first : first + width],
                     start=True,
                     stop=True,
                 )
                 banks.append(bank)
-            dp.append(banks)
+            return banks
 
-        ds_rows = [sb.tile([P, PACK, HALF], BF16, name=f"ds_rows{h}") for h in range(2)]
+        v_sel_words = []
+        for h in range(2):
+            sel = sb.tile([P, HALF], U32, name=("pool_scales", "do_bf1")[h], align_bytes=64)
+            nc.vector.tensor_copy(sel[:], pool_words[:].bitcast(U32).indirect(list_half(h)))
+            v_sel_words.append(sel)
 
-        def ds_row(h, t):
-            nc.vector.scalar_tensor_tensor(
-                ds_rows[h][:, t, :], dp[h][t][:], delta_raw[:, t : t + 1], p_half[h][:, t, :], SUBTRACT, MULT
-            )
+        def ds_row(rows, bank, t, p_row):
+            nc.vector.scalar_tensor_tensor(rows[:, t, :], bank[:], delta_raw[:, t : t + 1], p_row, SUBTRACT, MULT)
 
         ds_codes = sb.tile([P, N], U32, name="ds_codes", align_bytes=64)
         ds_scales = sb.tile([P, N], U8, name="ds_scales", align_bytes=64)
@@ -136,12 +126,8 @@ def tile_attend_bwd_kernel(tc, doT, v_words, v_scales, p, delta, qm, offs, out):
         def quantize_ds(first, words, width):
             quantize(ds_codes[:, first : first + width], ds_scales[:, first : first + width], words[:])
 
-        qm_bf = [sb.tile([P, P, PACK], BF16, name=f"qm_bf{c}", align_bytes=64) for c in range(2)]
         qm_codes = [sb.tile([P, P], U32, name=f"qm_codes{c}", align_bytes=64) for c in range(2)]
         qm_scales = [sb.tile([P, P], U8, name=f"qm_scales{c}", align_bytes=64) for c in range(2)]
-
-        def interleave_qm(c):
-            nc.scalar.copy(interleaved(qm_bf[c][:]), in_runs(qm_raw[:, :, c * P : (c + 1) * P]))
 
         def dk_product(c, first, width, bank):
             acc = ps.tile([P, width], F32, name=f"bank{bank}")
@@ -156,34 +142,49 @@ def tile_attend_bwd_kernel(tc, doT, v_words, v_scales, p, delta, qm, offs, out):
             )
             return acc
 
-        ds_first = sb.tile([P, HALF, PACK], BF16, name="ds_first", align_bytes=64)
-        ds_third = sb.tile([P, PIECE, PACK], BF16, name="ds_third", align_bytes=64)
-        ds_last = sb.tile([P, PIECE, PACK], BF16, name="ds_last", align_bytes=64)
-        for t in range(PACK):
-            ds_row(0, t)
-        interleave_qm(0)
-        nc.scalar.copy(interleaved(ds_first[:]), in_runs(ds_rows[0][:]))
-        interleave_qm(1)
-        ds_row(1, 0)
-        ds_row(1, 1)
-        quantize(qm_codes[0][:], qm_scales[0][:], qm_bf[0][:])
-        ds_row(1, 2)
-        quantize_ds(0, ds_first, HALF)
-        ds_row(1, 3)
-        nc.scalar.copy(interleaved(ds_third[:]), in_runs(ds_rows[1][:, :, 0:PIECE]))
-        nc.vector.tensor_copy(interleaved(ds_last[:]), in_runs(ds_rows[1][:, :, PIECE:HALF]))
-        acc_low = dk_product(0, 0, HALF, 0)
-        quantize_ds(HALF, ds_third, PIECE)
-        quantize_ds(HALF + PIECE, ds_last, PIECE)
+        piece_bf = []
+        for a in range(2):
+            cols = slice(a * PIECE, (a + 1) * PIECE)
+            banks = dp_products(v_sel_words[0][:, cols], a * PIECE, PIECE, PACK * a)
+            rows = sb.tile([P, PACK, PIECE], BF16, name=f"piece_rows{a}", align_bytes=64)
+            for t in range(PACK):
+                ds_row(rows, banks[t], t, p_half[0][:, t, cols])
+            words = sb.tile([P, PIECE, PACK], BF16, name=f"piece_bf{a}", align_bytes=64)
+            nc.scalar.copy(interleaved(words[:]), in_runs(rows[:]))
+            piece_bf.append(words)
 
-        dk_low = [sb.tile([P, HALF], F32, name=f"dk_low{h}") for h in range(2)]
-        dk_high = sb.tile([P, N], F32, name="dk_high")
-        nc.scalar.copy(dk_low[0][:], acc_low[:])
-        quantize(qm_codes[1][:], qm_scales[1][:], qm_bf[1][:])
-        nc.scalar.copy(dk_low[1][:], dk_product(0, HALF, HALF, 1)[:])
-        nc.vector.tensor_copy(windows[0][:].indirect(list_half(0)), dk_low[0][:])
-        nc.scalar.copy(dk_high[:], dk_product(1, 0, N, 2)[:])
-        nc.vector.tensor_copy(windows[0][:].indirect(list_half(1)), dk_low[1][:])
+        qm_bf0 = sb.tile([P, P, PACK], BF16, name="qm_bf0", align_bytes=64)
+        nc.gpsimd.tensor_scalar(qm_bf0[:], qm_raw[:, :, 0:P].rearrange("p t c -> p c t"), 1.0, 0.0, MULT, ADD)
+        qm_bf1 = sb.tile([P, P, PACK], BF16, name="piece_rows1", align_bytes=64)
+        nc.scalar.copy(interleaved(qm_bf1[:]), in_runs(qm_raw[:, :, P : 2 * P]))
+
+        banks = dp_products(v_sel_words[1][:], HALF, HALF, 0)
+        late_rows = sb.tile([P, PACK, HALF], BF16, name="late_rows", align_bytes=64)
+        ds_row(late_rows, banks[0], 0, p_half[1][:, 0, :])
+        ds_row(late_rows, banks[1], 1, p_half[1][:, 1, :])
+        quantize(qm_codes[0][:], qm_scales[0][:], qm_bf0[:])
+        quantize_ds(0, piece_bf[0], PIECE)
+        quantize_ds(PIECE, piece_bf[1], PIECE)
+        acc00 = dk_product(0, 0, HALF, 4)
+        ds_row(late_rows, banks[2], 2, p_half[1][:, 2, :])
+        ds_row(late_rows, banks[3], 3, p_half[1][:, 3, :])
+        quantize(qm_codes[1][:], qm_scales[1][:], qm_bf1[:])
+        acc10 = dk_product(1, 0, HALF, 5)
+
+        dk00 = sb.tile([P, HALF], F32, name="dk00")
+        nc.scalar.copy(dk00[:], acc00[:])
+        late_bf = sb.tile([P, HALF, PACK], BF16, name="late_bf", align_bytes=64)
+        nc.scalar.copy(interleaved(late_bf[:]), in_runs(late_rows[:]))
+        nc.vector.tensor_copy(windows[0][:].indirect(list_half(0)), dk00[:])
+        quantize_ds(HALF, late_bf, HALF)
+        dk1 = sb.tile([P, N], F32, name="late_rows", align_bytes=64)
+        nc.scalar.copy(dk1[:, 0:HALF], acc10[:])
+        dk01 = sb.tile([P, HALF], F32, name="dk01")
+        nc.scalar.copy(dk01[:], dk_product(0, HALF, HALF, 6)[:])
+        nc.scalar.copy(dk1[:, HALF:N], dk_product(1, HALF, HALF, 7)[:])
+        piece_cols = PIECE // 16
+        nc.vector.tensor_tensor(windows[1][:].indirect(offsets[:, 0:piece_cols]), dk1[:, 0:PIECE], zeros[:], ADD)
+        nc.vector.tensor_copy(windows[0][:].indirect(list_half(1)), dk01[:])
         nc.sync.dma_start(out[0:P, :], windows[0][:])
-        nc.vector.tensor_copy(windows[1][:].indirect(offsets[:]), dk_high[:])
+        nc.vector.tensor_copy(windows[1][:].indirect(offsets[:, piece_cols:LIST_COLS]), dk1[:, PIECE:N])
         nc.sync.dma_start(out[P : 2 * P, :], windows[1][:])

@@ -20,6 +20,7 @@ P = 128
 PACK = 4
 HALF = N // 2
 PIECE = HALF // 2
+COVER = 160
 LIST_COLS = N // 16
 SCALE_WORDS = T // 4
 RUN = 4
@@ -73,7 +74,7 @@ def tile_attend_bwd_kernel(tc, doT, v_words, v_scales, p, delta, qm, offs, out):
         nc.scalar.copy(warm[:, 1:2], warm[:, 0:1])
         nc.vector.memset(windows[0][:].bitcast(I32), 0)
         nc.gpsimd.memset(windows[1][:].bitcast(I32), 0)
-        zeros = sb.tile([P, PIECE], F32, name="zeros")
+        zeros = sb.tile([P, COVER], F32, name="zeros")
         nc.gpsimd.memset(zeros[:], 0.0)
 
         v_sel_scales = sb.tile([P, N], U8, name="v_sel_scales", align_bytes=64)
@@ -155,36 +156,40 @@ def tile_attend_bwd_kernel(tc, doT, v_words, v_scales, p, delta, qm, offs, out):
 
         qm_bf0 = sb.tile([P, P, PACK], BF16, name="qm_bf0", align_bytes=64)
         nc.gpsimd.tensor_scalar(qm_bf0[:], qm_raw[:, :, 0:P].rearrange("p t c -> p c t"), 1.0, 0.0, MULT, ADD)
-        qm_bf1 = sb.tile([P, P, PACK], BF16, name="piece_rows1", align_bytes=64)
-        nc.scalar.copy(interleaved(qm_bf1[:]), in_runs(qm_raw[:, :, P : 2 * P]))
+        qm_bf1 = sb.tile([P, P, PACK], BF16, name="qm_bf1", align_bytes=64)
+        nc.gpsimd.tensor_scalar(qm_bf1[:], qm_raw[:, :, P : 2 * P].rearrange("p t c -> p c t"), 1.0, 0.0, MULT, ADD)
 
         banks = dp_products(v_sel_words[1][:], HALF, HALF, 0)
         late_rows = sb.tile([P, PACK, HALF], BF16, name="late_rows", align_bytes=64)
         ds_row(late_rows, banks[0], 0, p_half[1][:, 0, :])
         ds_row(late_rows, banks[1], 1, p_half[1][:, 1, :])
         quantize(qm_codes[0][:], qm_scales[0][:], qm_bf0[:])
-        quantize_ds(0, piece_bf[0], PIECE)
-        quantize_ds(PIECE, piece_bf[1], PIECE)
-        acc00 = dk_product(0, 0, HALF, 4)
+        dk00 = sb.tile([P, HALF], F32, name="dk00")
+        for a in range(2):
+            quantize_ds(a * PIECE, piece_bf[a], PIECE)
+            nc.scalar.copy(dk00[:, a * PIECE : (a + 1) * PIECE], dk_product(0, a * PIECE, PIECE, 4 + a)[:])
         ds_row(late_rows, banks[2], 2, p_half[1][:, 2, :])
         ds_row(late_rows, banks[3], 3, p_half[1][:, 3, :])
         quantize(qm_codes[1][:], qm_scales[1][:], qm_bf1[:])
-        acc10 = dk_product(1, 0, HALF, 5)
+        acc10 = dk_product(1, 0, HALF, 6)
 
-        dk00 = sb.tile([P, HALF], F32, name="dk00")
-        nc.scalar.copy(dk00[:], acc00[:])
-        late_bf = sb.tile([P, HALF, PACK], BF16, name="late_bf", align_bytes=64)
-        nc.scalar.copy(interleaved(late_bf[:]), in_runs(late_rows[:]))
+        late_bf = []
+        for a in range(2):
+            words = sb.tile([P, PIECE, PACK], BF16, name=f"late_bf{a}", align_bytes=64)
+            nc.scalar.copy(interleaved(words[:]), in_runs(late_rows[:, :, a * PIECE : (a + 1) * PIECE]))
+            late_bf.append(words)
         nc.vector.tensor_copy(windows[0][:].indirect(list_half(0)), dk00[:])
-        quantize_ds(HALF, late_bf, HALF)
-        dk1 = sb.tile([P, N], F32, name="late_rows", align_bytes=64)
+        dk1 = sb.tile([P, N], F32, name="p_half1")
         nc.scalar.copy(dk1[:, 0:HALF], acc10[:])
         dk01 = sb.tile([P, HALF], F32, name="dk01")
-        nc.scalar.copy(dk01[:], dk_product(0, HALF, HALF, 6)[:])
+        for a in range(2):
+            first = HALF + a * PIECE
+            quantize_ds(first, late_bf[a], PIECE)
+            nc.scalar.copy(dk01[:, a * PIECE : (a + 1) * PIECE], dk_product(0, first, PIECE, a)[:])
         nc.scalar.copy(dk1[:, HALF:N], dk_product(1, HALF, HALF, 7)[:])
-        piece_cols = PIECE // 16
-        nc.vector.tensor_tensor(windows[1][:].indirect(offsets[:, 0:piece_cols]), dk1[:, 0:PIECE], zeros[:], ADD)
+        piece_cols = COVER // 16
+        nc.vector.tensor_tensor(windows[1][:].indirect(offsets[:, 0:piece_cols]), dk1[:, 0:COVER], zeros[:], ADD)
         nc.vector.tensor_copy(windows[0][:].indirect(list_half(1)), dk01[:])
         nc.sync.dma_start(out[0:P, :], windows[0][:])
-        nc.vector.tensor_copy(windows[1][:].indirect(offsets[:, piece_cols:LIST_COLS]), dk1[:, PIECE:N])
+        nc.vector.tensor_copy(windows[1][:].indirect(offsets[:, piece_cols:LIST_COLS]), dk1[:, COVER:N])
         nc.sync.dma_start(out[P : 2 * P, :], windows[1][:])

@@ -156,8 +156,8 @@ def tile_attend_bwd_kernel(tc, doT, v_words, v_scales, p, delta, qm, offs, out):
 
         qm_bf0 = sb.tile([P, P, PACK], BF16, name="qm_bf0", align_bytes=64)
         nc.gpsimd.tensor_scalar(qm_bf0[:], qm_raw[:, :, 0:P].rearrange("p t c -> p c t"), 1.0, 0.0, MULT, ADD)
-        qm_bf1 = sb.tile([P, P, PACK], BF16, name="qm_bf1", align_bytes=64)
-        nc.gpsimd.tensor_scalar(qm_bf1[:], qm_raw[:, :, P : 2 * P].rearrange("p t c -> p c t"), 1.0, 0.0, MULT, ADD)
+        qm_bf1 = sb.tile([P, P, PACK], BF16, name="piece_rows1", align_bytes=64)
+        nc.scalar.copy(interleaved(qm_bf1[:]), in_runs(qm_raw[:, :, P : 2 * P]))
 
         banks = dp_products(v_sel_words[1][:], HALF, HALF, 0)
         late_rows = sb.tile([P, PACK, HALF], BF16, name="late_rows", align_bytes=64)

@@ -155,19 +155,20 @@ def tile_attend_bwd_kernel(tc, doT, v_words, v_scales, p, delta, qm, offs, out):
             piece_bf.append(words)
 
         qm_bf0 = sb.tile([P, P, PACK], BF16, name="qm_bf0", align_bytes=64)
-        nc.gpsimd.tensor_scalar(qm_bf0[:], qm_raw[:, :, 0:P].rearrange("p t c -> p c t"), 1.0, 0.0, MULT, ADD)
+        nc.vector.tensor_copy(interleaved(qm_bf0[:]), in_runs(qm_raw[:, :, 0:P]))
         qm_bf1 = sb.tile([P, P, PACK], BF16, name="piece_rows1", align_bytes=64)
         nc.scalar.copy(interleaved(qm_bf1[:]), in_runs(qm_raw[:, :, P : 2 * P]))
 
         banks = dp_products(v_sel_words[1][:], HALF, HALF, 0)
         late_rows = sb.tile([P, PACK, HALF], BF16, name="late_rows", align_bytes=64)
-        ds_row(late_rows, banks[0], 0, p_half[1][:, 0, :])
-        ds_row(late_rows, banks[1], 1, p_half[1][:, 1, :])
+        quantize_ds(0, piece_bf[0], PIECE)
         quantize(qm_codes[0][:], qm_scales[0][:], qm_bf0[:])
+        quantize_ds(PIECE, piece_bf[1], PIECE)
         dk00 = sb.tile([P, HALF], F32, name="dk00")
         for a in range(2):
-            quantize_ds(a * PIECE, piece_bf[a], PIECE)
             nc.scalar.copy(dk00[:, a * PIECE : (a + 1) * PIECE], dk_product(0, a * PIECE, PIECE, 4 + a)[:])
+        ds_row(late_rows, banks[0], 0, p_half[1][:, 0, :])
+        ds_row(late_rows, banks[1], 1, p_half[1][:, 1, :])
         ds_row(late_rows, banks[2], 2, p_half[1][:, 2, :])
         ds_row(late_rows, banks[3], 3, p_half[1][:, 3, :])
         quantize(qm_codes[1][:], qm_scales[1][:], qm_bf1[:])

@@ -14,13 +14,13 @@ U8 = mybir.dt.uint8
 FP8X4 = mybir.dt.float8_e4m3fn_x4
 MULT = mybir.AluOpType.mult
 SUBTRACT = mybir.AluOpType.subtract
-ADD = mybir.AluOpType.add
+IDENTITY = mybir.ActivationFunctionType.Identity
+COPY = mybir.ActivationFunctionType.Copy
 
 P = 128
 PACK = 4
 HALF = N // 2
 PIECE = HALF // 2
-COVER = 160
 LIST_COLS = N // 16
 SCALE_WORDS = T // 4
 RUN = 4
@@ -49,8 +49,8 @@ def tile_attend_bwd_kernel(tc, doT, v_words, v_scales, p, delta, qm, offs, out):
         delta_raw = sb.tile([P, PACK], F32, name="delta_raw")
         windows = [sb.tile([P, T], F32, name=f"window{c}") for c in range(2)]
 
-        def list_half(h):
-            return offsets[:, h * (LIST_COLS // 2) : (h + 1) * (LIST_COLS // 2)]
+        def slots(first, width):
+            return offsets[:, first // 16 : (first + width) // 16]
 
         nc.gpsimd.memset(pool_scales[:], 0)
 
@@ -66,16 +66,13 @@ def tile_attend_bwd_kernel(tc, doT, v_words, v_scales, p, delta, qm, offs, out):
         p_rows = p[0].rearrange("(p t) n -> p t n", t=PACK)
         nc.sync.dma_start(p_half[0][:], p_rows[:, :, 0:HALF])
         nc.sync.dma_start(qm_raw[:], qm[0].rearrange("(p t) d -> p t d", t=PACK))
-        for u in range(2):
-            nc.sync.dma_start(p_half[1][:, 2 * u : 2 * u + 2, :], p_rows[:, 2 * u : 2 * u + 2, HALF:N])
+        nc.sync.dma_start(p_half[1][:], p_rows[:, :, HALF:N])
 
         warm = sb.tile([P, 2], F32, name="warm")
         nc.vector.memset(warm[:, 0:1], 0.0)
         nc.scalar.copy(warm[:, 1:2], warm[:, 0:1])
         nc.vector.memset(windows[0][:].bitcast(I32), 0)
         nc.gpsimd.memset(windows[1][:].bitcast(I32), 0)
-        zeros = sb.tile([P, COVER], F32, name="zeros")
-        nc.gpsimd.memset(zeros[:], 0.0)
 
         v_sel_scales = sb.tile([P, N], U8, name="v_sel_scales", align_bytes=64)
         nc.vector.tensor_copy(v_sel_scales[:], pool_scales[:].bitcast(U8).indirect(offsets[:]))
@@ -92,48 +89,56 @@ def tile_attend_bwd_kernel(tc, doT, v_words, v_scales, p, delta, qm, offs, out):
             do_codes.append(codes)
             do_scales.append(scales)
 
-        def dp_products(words, first, width, bank0):
-            banks = []
-            for t in range(PACK):
-                u, w = divmod(t, 2)
-                bank = ps.tile([P, width], F32, name=f"bank{bank0 + t}")
-                nc.tensor.matmul_mx(
-                    bank[:],
-                    lhsT=do_codes[u][:, w * P : (w + 1) * P].bitcast(FP8X4),
-                    lhsT_scale=do_scales[u][:, w * P : (w + 1) * P],
-                    rhs=words.bitcast(FP8X4),
-                    rhs_scale=v_sel_scales[:, first : first + width],
-                    start=True,
-                    stop=True,
-                )
-                banks.append(bank)
-            return banks
+        minus_delta = sb.tile([P, PACK], F32, name="minus_delta")
+        nc.scalar.mul(minus_delta[:], delta_raw[:], -1.0)
 
-        v_sel_words = []
-        for h in range(2):
-            sel = sb.tile([P, HALF], U32, name=("pool_scales", "do_bf1")[h], align_bytes=64)
-            nc.vector.tensor_copy(sel[:], pool_words[:].bitcast(U32).indirect(list_half(h)))
-            v_sel_words.append(sel)
+        banks = [ps.tile([P, N], F32, name=f"bank{b}") for b in range(8)]
+        gathered = []
+        for a, (first, width) in enumerate([(0, PIECE), (PIECE, PIECE), (HALF, HALF)]):
+            sel = sb.tile([P, width], U32, name=("pool_scales", "do_bf1", "sel2")[a], align_bytes=64)
+            nc.vector.tensor_copy(sel[:], pool_words[:].bitcast(U32).indirect(slots(first, width)))
+            gathered.append(sel)
 
-        def ds_row(rows, bank, t, p_row):
-            nc.vector.scalar_tensor_tensor(rows[:, t, :], bank[:], delta_raw[:, t : t + 1], p_row, SUBTRACT, MULT)
+        def dp_product(words, first, width, t, bank_no):
+            u, w = divmod(t, 2)
+            bank = banks[bank_no][:, 0:width]
+            nc.tensor.matmul_mx(
+                bank,
+                lhsT=do_codes[u][:, w * P : (w + 1) * P].bitcast(FP8X4),
+                lhsT_scale=do_scales[u][:, w * P : (w + 1) * P],
+                rhs=words[:].bitcast(FP8X4),
+                rhs_scale=v_sel_scales[:, first : first + width],
+                start=True,
+                stop=True,
+            )
+            return bank
 
-        ds_codes = sb.tile([P, N], U32, name="ds_codes", align_bytes=64)
-        ds_scales = sb.tile([P, N], U8, name="ds_scales", align_bytes=64)
+        def centre(rows, t, bank):
+            nc.scalar.activation(rows[:, t, :], bank, IDENTITY, bias=minus_delta[:, t : t + 1])
 
         def quantize(codes, scales, words):
             nc.vector.quantize_mx(codes.bitcast(FP8X4), scales, words.rearrange("p n t -> p (n t)"))
 
-        def quantize_ds(first, words, width):
-            quantize(ds_codes[:, first : first + width], ds_scales[:, first : first + width], words[:])
-
+        early_bf = sb.tile([P, 3 * PIECE, PACK], BF16, name="early_bf", align_bytes=64)
+        ds_bf = [early_bf[:, 0:PIECE, :], early_bf[:, PIECE:HALF, :]]
+        qm_bf0 = early_bf[:, HALF : HALF + P, :]
+        late_bf = early_bf[:, PIECE : PIECE + HALF, :]
+        qm_bf1 = sb.tile([P, P, PACK], BF16, name="qm_bf1", align_bytes=64)
+        ds_codes = sb.tile([P, N], U32, name="ds_codes", align_bytes=64)
+        ds_scales = sb.tile([P, N], U8, name="ds_scales", align_bytes=64)
         qm_codes = [sb.tile([P, P], U32, name=f"qm_codes{c}", align_bytes=64) for c in range(2)]
         qm_scales = [sb.tile([P, P], U8, name=f"qm_scales{c}", align_bytes=64) for c in range(2)]
 
-        def dk_product(c, first, width, bank):
-            acc = ps.tile([P, width], F32, name=f"bank{bank}")
+        def weigh(words, centred_rows, p_rows_sb):
+            nc.vector.tensor_tensor(interleaved(words), in_runs(centred_rows), in_runs(p_rows_sb), MULT)
+
+        def quantize_ds(first, width, words):
+            quantize(ds_codes[:, first : first + width], ds_scales[:, first : first + width], words)
+
+        def dk_product(c, first, width, bank_no):
+            acc = banks[bank_no][:, 0:width]
             nc.tensor.matmul_mx(
-                acc[:],
+                acc,
                 lhsT=qm_codes[c][:].bitcast(FP8X4),
                 lhsT_scale=qm_scales[c][:],
                 rhs=ds_codes[:, first : first + width].bitcast(FP8X4),
@@ -143,54 +148,41 @@ def tile_attend_bwd_kernel(tc, doT, v_words, v_scales, p, delta, qm, offs, out):
             )
             return acc
 
-        piece_bf = []
-        for a in range(2):
-            cols = slice(a * PIECE, (a + 1) * PIECE)
-            banks = dp_products(v_sel_words[0][:, cols], a * PIECE, PIECE, PACK * a)
-            rows = sb.tile([P, PACK, PIECE], BF16, name=f"piece_rows{a}", align_bytes=64)
-            for t in range(PACK):
-                ds_row(rows, banks[t], t, p_half[0][:, t, cols])
-            words = sb.tile([P, PIECE, PACK], BF16, name=f"piece_bf{a}", align_bytes=64)
-            nc.scalar.copy(interleaved(words[:]), in_runs(rows[:]))
-            piece_bf.append(words)
-
-        qm_bf0 = sb.tile([P, P, PACK], BF16, name="qm_bf0", align_bytes=64)
-        nc.vector.tensor_copy(interleaved(qm_bf0[:]), in_runs(qm_raw[:, :, 0:P]))
-        qm_bf1 = sb.tile([P, P, PACK], BF16, name="piece_rows1", align_bytes=64)
+        rows0 = sb.tile([P, PACK, PIECE], BF16, name="rows0", align_bytes=64)
+        for t in range(PACK):
+            bank = dp_product(gathered[0], 0, PIECE, t, t)
+            nc.vector.scalar_tensor_tensor(
+                rows0[:, t, :], bank, delta_raw[:, t : t + 1], p_half[0][:, t, 0:PIECE], SUBTRACT, MULT
+            )
+        centred1 = sb.tile([P, PACK, PIECE], F32, name="centred1")
+        for t in range(PACK):
+            centre(centred1, t, dp_product(gathered[1], PIECE, PIECE, t, PACK + t))
+        nc.scalar.copy(interleaved(ds_bf[0]), in_runs(rows0[:]))
+        centred_late = sb.tile([P, PACK, HALF], F32, name="centred_late")
+        for t in range(PACK):
+            centre(centred_late, t, dp_product(gathered[2], HALF, HALF, t, t))
         nc.scalar.copy(interleaved(qm_bf1[:]), in_runs(qm_raw[:, :, P : 2 * P]))
 
-        banks = dp_products(v_sel_words[1][:], HALF, HALF, 0)
-        late_rows = sb.tile([P, PACK, HALF], BF16, name="late_rows", align_bytes=64)
-        quantize_ds(0, piece_bf[0], PIECE)
-        quantize(qm_codes[0][:], qm_scales[0][:], qm_bf0[:])
-        quantize_ds(PIECE, piece_bf[1], PIECE)
-        dk00 = sb.tile([P, HALF], F32, name="dk00")
-        for a in range(2):
-            nc.scalar.copy(dk00[:, a * PIECE : (a + 1) * PIECE], dk_product(0, a * PIECE, PIECE, 4 + a)[:])
-        ds_row(late_rows, banks[0], 0, p_half[1][:, 0, :])
-        ds_row(late_rows, banks[1], 1, p_half[1][:, 1, :])
-        ds_row(late_rows, banks[2], 2, p_half[1][:, 2, :])
-        ds_row(late_rows, banks[3], 3, p_half[1][:, 3, :])
-        quantize(qm_codes[1][:], qm_scales[1][:], qm_bf1[:])
-        acc10 = dk_product(1, 0, HALF, 6)
+        weigh(ds_bf[1], centred1[:], p_half[0][:, :, PIECE:HALF])
+        nc.vector.tensor_copy(interleaved(qm_bf0), in_runs(qm_raw[:, :, 0:P]))
+        quantize_ds(PIECE, PIECE, ds_bf[1])
+        quantize(qm_codes[0][:], qm_scales[0][:], qm_bf0)
+        quantize_ds(0, PIECE, ds_bf[0])
+        dk0 = [sb.tile([P, HALF], F32, name=f"dk0{h}") for h in range(2)]
+        dk1 = [sb.tile([P, HALF], F32, name=f"dk1{h}") for h in range(2)]
+        for a in (1, 0):
+            nc.scalar.copy(dk0[0][:, a * PIECE : (a + 1) * PIECE], dk_product(0, a * PIECE, PIECE, PACK + a))
+        nc.scalar.activation(windows[0][:].indirect(slots(0, HALF)), dk0[0][:], COPY)
 
-        late_bf = []
-        for a in range(2):
-            words = sb.tile([P, PIECE, PACK], BF16, name=f"late_bf{a}", align_bytes=64)
-            nc.scalar.copy(interleaved(words[:]), in_runs(late_rows[:, :, a * PIECE : (a + 1) * PIECE]))
-            late_bf.append(words)
-        nc.vector.tensor_copy(windows[0][:].indirect(list_half(0)), dk00[:])
-        dk1 = sb.tile([P, N], F32, name="p_half1")
-        nc.scalar.copy(dk1[:, 0:HALF], acc10[:])
-        dk01 = sb.tile([P, HALF], F32, name="dk01")
-        for a in range(2):
-            first = HALF + a * PIECE
-            quantize_ds(first, late_bf[a], PIECE)
-            nc.scalar.copy(dk01[:, a * PIECE : (a + 1) * PIECE], dk_product(0, first, PIECE, a)[:])
-        nc.scalar.copy(dk1[:, HALF:N], dk_product(1, HALF, HALF, 7)[:])
-        piece_cols = COVER // 16
-        nc.vector.tensor_tensor(windows[1][:].indirect(offsets[:, 0:piece_cols]), dk1[:, 0:COVER], zeros[:], ADD)
-        nc.vector.tensor_copy(windows[0][:].indirect(list_half(1)), dk01[:])
+        weigh(late_bf, centred_late[:], p_half[1][:])
+        quantize(qm_codes[1][:], qm_scales[1][:], qm_bf1[:])
+        quantize_ds(HALF, HALF, late_bf)
+        nc.vector.tensor_copy(dk1[0][:], dk_product(1, 0, HALF, 6))
+        nc.vector.tensor_copy(dk0[1][:], dk_product(0, HALF, HALF, 7))
+        nc.scalar.activation(windows[0][:].indirect(slots(HALF, HALF)), dk0[1][:], COPY)
         nc.sync.dma_start(out[0:P, :], windows[0][:])
-        nc.vector.tensor_copy(windows[1][:].indirect(offsets[:, piece_cols:LIST_COLS]), dk1[:, COVER:N])
+
+        nc.vector.tensor_copy(windows[1][:].indirect(slots(0, HALF)), dk1[0][:])
+        nc.scalar.copy(dk1[1][:], dk_product(1, HALF, HALF, 7))
+        nc.vector.tensor_copy(windows[1][:].indirect(slots(HALF, HALF)), dk1[1][:])
         nc.sync.dma_start(out[P : 2 * P, :], windows[1][:])

@@ -119,14 +119,12 @@ def tile_attend_bwd_kernel(tc, doT, v_words, v_scales, p, delta, qm, offs, out):
         def quantize(codes, scales, words):
             nc.vector.quantize_mx(codes.bitcast(FP8X4), scales, words.rearrange("p n t -> p (n t)"))
 
-        early_bf = sb.tile([P, 3 * PIECE, PACK], BF16, name="early_bf", align_bytes=64)
-        ds_bf = [early_bf[:, 0:PIECE, :], early_bf[:, PIECE:HALF, :]]
-        qm_bf0 = early_bf[:, HALF : HALF + P, :]
-        late_bf = early_bf[:, PIECE : PIECE + HALF, :]
+        ds_bf = [sb.tile([P, PIECE, PACK], BF16, name=f"ds_bf{a}", align_bytes=64)[:] for a in range(2)]
+        qm_bf0 = sb.tile([P, P, PACK], BF16, name="qm_bf0", align_bytes=64)[:]
         qm_bf1 = sb.tile([P, P, PACK], BF16, name="qm_bf1", align_bytes=64)
         ds_codes = sb.tile([P, N], U32, name="ds_codes", align_bytes=64)
         ds_scales = sb.tile([P, N], U8, name="ds_scales", align_bytes=64)
-        qm_codes = [sb.tile([P, P], U32, name=f"qm_codes{c}", align_bytes=64) for c in range(2)]
+        qm_codes = [sb.tile([P, P], U32, name="qm_codes0", align_bytes=64)]
         qm_scales = [sb.tile([P, P], U8, name=f"qm_scales{c}", align_bytes=64) for c in range(2)]
 
         def weigh(words, centred_rows, p_rows_sb):
@@ -169,20 +167,26 @@ def tile_attend_bwd_kernel(tc, doT, v_words, v_scales, p, delta, qm, offs, out):
         quantize(qm_codes[0][:], qm_scales[0][:], qm_bf0)
         quantize_ds(0, PIECE, ds_bf[0])
         dk0 = [sb.tile([P, HALF], F32, name=f"dk0{h}") for h in range(2)]
-        dk1 = [sb.tile([P, HALF], F32, name=f"dk1{h}") for h in range(2)]
         for a in (1, 0):
             nc.scalar.copy(dk0[0][:, a * PIECE : (a + 1) * PIECE], dk_product(0, a * PIECE, PIECE, PACK + a))
         nc.scalar.activation(windows[0][:].indirect(slots(0, HALF)), dk0[0][:], COPY)
 
-        weigh(late_bf, centred_late[:], p_half[1][:])
+        pieces = [slice(a * PIECE, (a + 1) * PIECE) for a in range(2)]
+        late_bf = [sb.tile([P, PIECE, PACK], BF16, name=tag, align_bytes=64)[:] for tag in ("qm_bf0", "ds_bf1")]
+        for a, cols in enumerate(pieces):
+            weigh(late_bf[a], centred_late[:, :, cols], p_half[1][:, :, cols])
+        for a in range(2):
+            quantize_ds(HALF + a * PIECE, PIECE, late_bf[a])
+        qm_codes.append(sb.tile([P, P], U32, name="qm_bf0", align_bytes=64))
         quantize(qm_codes[1][:], qm_scales[1][:], qm_bf1[:])
-        quantize_ds(HALF, HALF, late_bf)
-        nc.vector.tensor_copy(dk1[0][:], dk_product(1, 0, HALF, 6))
-        nc.vector.tensor_copy(dk0[1][:], dk_product(0, HALF, HALF, 7))
+        for a, cols in enumerate(pieces):
+            nc.vector.tensor_copy(dk0[1][:, cols], dk_product(0, HALF + a * PIECE, PIECE, 6 + a))
         nc.scalar.activation(windows[0][:].indirect(slots(HALF, HALF)), dk0[1][:], COPY)
         nc.sync.dma_start(out[0:P, :], windows[0][:])
 
-        nc.vector.tensor_copy(windows[1][:].indirect(slots(0, HALF)), dk1[0][:])
-        nc.scalar.copy(dk1[1][:], dk_product(1, HALF, HALF, 7))
-        nc.vector.tensor_copy(windows[1][:].indirect(slots(HALF, HALF)), dk1[1][:])
+        dk1_all = sb.tile([P, N], F32, name="dk1_all")
+        for h in range(2):
+            nc.vector.tensor_copy(dk1_all[:, h * HALF : (h + 1) * HALF], dk_product(1, h * HALF, HALF, h))
+        for h in range(2):
+            nc.vector.tensor_copy(windows[1][:].indirect(slots(h * HALF, HALF)), dk1_all[:, h * HALF : (h + 1) * HALF])
         nc.sync.dma_start(out[P : 2 * P, :], windows[1][:])

@@ -13,7 +13,6 @@ U16 = mybir.dt.uint16
 U8 = mybir.dt.uint8
 FP8X4 = mybir.dt.float8_e4m3fn_x4
 MULT = mybir.AluOpType.mult
-SUBTRACT = mybir.AluOpType.subtract
 IDENTITY = mybir.ActivationFunctionType.Identity
 COPY = mybir.ActivationFunctionType.Copy
 
@@ -44,7 +43,7 @@ def tile_attend_bwd_kernel(tc, doT, v_words, v_scales, p, delta, qm, offs, out):
         pool_scales = sb.tile([P, SCALE_WORDS], I32, name="pool_scales", align_bytes=64)
         pool_words = sb.tile([P, T], I32, name="pool_words")
         do_raw = sb.tile([P, PACK, NQ], F32, name="do_raw")
-        qm_raw = sb.tile([P, PACK, D], F32, name="qm_raw")
+        qm_raw = [sb.tile([P, PACK, P], F32, name=f"qm_raw{c}") for c in range(2)]
         p_half = [sb.tile([P, PACK, HALF], F32, name=f"p_half{h}") for h in range(2)]
         delta_raw = sb.tile([P, PACK], F32, name="delta_raw")
         windows = [sb.tile([P, T], F32, name=f"window{c}") for c in range(2)]
@@ -64,9 +63,11 @@ def tile_attend_bwd_kernel(tc, doT, v_words, v_scales, p, delta, qm, offs, out):
         nc.sync.dma_start(pool_words[:], v_words[0].rearrange("p n r -> p (n r)").bitcast(I32))
         nc.sync.dma_start(delta_raw[:], delta[0].rearrange("(p t) o -> p (t o)", t=PACK))
         p_rows = p[0].rearrange("(p t) n -> p t n", t=PACK)
+        qm_rows = qm[0].rearrange("(p t) d -> p t d", t=PACK)
+        nc.sync.dma_start(qm_raw[0][:], qm_rows[:, :, 0:P])
         nc.sync.dma_start(p_half[0][:], p_rows[:, :, 0:HALF])
-        nc.sync.dma_start(qm_raw[:], qm[0].rearrange("(p t) d -> p t d", t=PACK))
         nc.sync.dma_start(p_half[1][:], p_rows[:, :, HALF:N])
+        nc.sync.dma_start(qm_raw[1][:], qm_rows[:, :, P:D])
 
         warm = sb.tile([P, 2], F32, name="warm")
         nc.vector.memset(warm[:, 0:1], 0.0)
@@ -121,10 +122,9 @@ def tile_attend_bwd_kernel(tc, doT, v_words, v_scales, p, delta, qm, offs, out):
 
         ds_bf = [sb.tile([P, PIECE, PACK], BF16, name=f"ds_bf{a}", align_bytes=64)[:] for a in range(2)]
         qm_bf0 = sb.tile([P, P, PACK], BF16, name="qm_bf0", align_bytes=64)[:]
-        qm_bf1 = sb.tile([P, P, PACK], BF16, name="qm_bf1", align_bytes=64)
         ds_codes = sb.tile([P, N], U32, name="ds_codes", align_bytes=64)
         ds_scales = sb.tile([P, N], U8, name="ds_scales", align_bytes=64)
-        qm_codes = [sb.tile([P, P], U32, name="qm_codes0", align_bytes=64)]
+        qm_codes = [sb.tile([P, P], U32, name=f"qm_codes{c}", align_bytes=64) for c in range(2)]
         qm_scales = [sb.tile([P, P], U8, name=f"qm_scales{c}", align_bytes=64) for c in range(2)]
 
         def weigh(words, centred_rows, p_rows_sb):
@@ -146,47 +146,43 @@ def tile_attend_bwd_kernel(tc, doT, v_words, v_scales, p, delta, qm, offs, out):
             )
             return acc
 
-        rows0 = sb.tile([P, PACK, PIECE], BF16, name="rows0", align_bytes=64)
-        for t in range(PACK):
-            bank = dp_product(gathered[0], 0, PIECE, t, t)
-            nc.vector.scalar_tensor_tensor(
-                rows0[:, t, :], bank, delta_raw[:, t : t + 1], p_half[0][:, t, 0:PIECE], SUBTRACT, MULT
-            )
-        centred1 = sb.tile([P, PACK, PIECE], F32, name="centred1")
-        for t in range(PACK):
-            centre(centred1, t, dp_product(gathered[1], PIECE, PIECE, t, PACK + t))
-        nc.scalar.copy(interleaved(ds_bf[0]), in_runs(rows0[:]))
+        nc.vector.tensor_copy(interleaved(qm_bf0), in_runs(qm_raw[0][:]))
+        quantize(qm_codes[0][:], qm_scales[0][:], qm_bf0)
+        centred = [sb.tile([P, PACK, PIECE], F32, name=f"centred{a}", align_bytes=64) for a in range(2)]
+        for a in range(2):
+            for t in range(PACK):
+                centre(centred[a], t, dp_product(gathered[a], a * PIECE, PIECE, t, PACK * a + t))
         centred_late = sb.tile([P, PACK, HALF], F32, name="centred_late")
         for t in range(PACK):
             centre(centred_late, t, dp_product(gathered[2], HALF, HALF, t, t))
-        nc.scalar.copy(interleaved(qm_bf1[:]), in_runs(qm_raw[:, :, P : 2 * P]))
 
-        weigh(ds_bf[1], centred1[:], p_half[0][:, :, PIECE:HALF])
-        nc.vector.tensor_copy(interleaved(qm_bf0), in_runs(qm_raw[:, :, 0:P]))
-        quantize_ds(PIECE, PIECE, ds_bf[1])
-        quantize(qm_codes[0][:], qm_scales[0][:], qm_bf0)
-        quantize_ds(0, PIECE, ds_bf[0])
+        for a in range(2):
+            weigh(ds_bf[a], centred[a][:], p_half[0][:, :, a * PIECE : (a + 1) * PIECE])
+        for a in range(2):
+            quantize_ds(a * PIECE, PIECE, ds_bf[a])
+        qm_bf1 = sb.tile([P, P, PACK], BF16, name="centred0", align_bytes=64)
+        nc.scalar.copy(interleaved(qm_bf1[:, 0 : P // 2, :]), in_runs(qm_raw[1][:, :, 0 : P // 2]))
+        nc.vector.tensor_copy(interleaved(qm_bf1[:, P // 2 : P, :]), in_runs(qm_raw[1][:, :, P // 2 : P]))
         dk0 = [sb.tile([P, HALF], F32, name=f"dk0{h}") for h in range(2)]
-        for a in (1, 0):
+        for a in range(2):
             nc.scalar.copy(dk0[0][:, a * PIECE : (a + 1) * PIECE], dk_product(0, a * PIECE, PIECE, PACK + a))
         nc.scalar.activation(windows[0][:].indirect(slots(0, HALF)), dk0[0][:], COPY)
 
         pieces = [slice(a * PIECE, (a + 1) * PIECE) for a in range(2)]
-        late_bf = [sb.tile([P, PIECE, PACK], BF16, name=tag, align_bytes=64)[:] for tag in ("qm_bf0", "ds_bf1")]
-        for a, cols in enumerate(pieces):
-            weigh(late_bf[a], centred_late[:, :, cols], p_half[1][:, :, cols])
+        late_bf = [sb.tile([P, PIECE, PACK], BF16, name=tag, align_bytes=64)[:] for tag in ("ds_bf0", "ds_bf1")]
+        weigh(late_bf[0], centred_late[:, :, pieces[0]], p_half[1][:, :, pieces[0]])
+        quantize(qm_codes[1][:], qm_scales[1][:], qm_bf1[:])
+        weigh(late_bf[1], centred_late[:, :, pieces[1]], p_half[1][:, :, pieces[1]])
         for a in range(2):
             quantize_ds(HALF + a * PIECE, PIECE, late_bf[a])
-        qm_codes.append(sb.tile([P, P], U32, name="qm_bf0", align_bytes=64))
-        quantize(qm_codes[1][:], qm_scales[1][:], qm_bf1[:])
+        dk1_all = sb.tile([P, N], F32, name="dk1_all")
+        nc.vector.tensor_copy(dk1_all[:, 0:HALF], dk_product(1, 0, HALF, 0))
         for a, cols in enumerate(pieces):
             nc.vector.tensor_copy(dk0[1][:, cols], dk_product(0, HALF + a * PIECE, PIECE, 6 + a))
         nc.scalar.activation(windows[0][:].indirect(slots(HALF, HALF)), dk0[1][:], COPY)
         nc.sync.dma_start(out[0:P, :], windows[0][:])
 
-        dk1_all = sb.tile([P, N], F32, name="dk1_all")
-        for h in range(2):
-            nc.vector.tensor_copy(dk1_all[:, h * HALF : (h + 1) * HALF], dk_product(1, h * HALF, HALF, h))
+        nc.vector.tensor_copy(dk1_all[:, HALF:N], dk_product(1, HALF, HALF, 1))
         for h in range(2):
             nc.vector.tensor_copy(windows[1][:].indirect(slots(h * HALF, HALF)), dk1_all[:, h * HALF : (h + 1) * HALF])
         nc.sync.dma_start(out[P : 2 * P, :], windows[1][:])

@@ -18,8 +18,10 @@ COPY = mybir.ActivationFunctionType.Copy
 
 P = 128
 PACK = 4
+DMA_ALIGN = 256
 HALF = N // 2
 PIECE = HALF // 2
+QM_SHARE = 32
 LIST_COLS = N // 16
 SCALE_WORDS = T // 4
 RUN = 4
@@ -40,13 +42,13 @@ def tile_attend_bwd_kernel(tc, doT, v_words, v_scales, p, delta, qm, offs, out):
         ps = ctx.enter_context(tc.psum_pool(name="ps", bufs=1))
 
         offsets = sb.tile([P, LIST_COLS], U16, name="offsets")
-        pool_scales = sb.tile([P, SCALE_WORDS], I32, name="pool_scales", align_bytes=64)
-        pool_words = sb.tile([P, T], I32, name="pool_words")
-        do_raw = sb.tile([P, PACK, NQ], F32, name="do_raw")
-        qm_raw = [sb.tile([P, PACK, P], F32, name=f"qm_raw{c}") for c in range(2)]
-        p_half = [sb.tile([P, PACK, HALF], F32, name=f"p_half{h}") for h in range(2)]
+        pool_scales = sb.tile([P, SCALE_WORDS], I32, name="pool_scales", align_bytes=DMA_ALIGN)
+        pool_words = sb.tile([P, T], I32, name="pool_words", align_bytes=DMA_ALIGN)
+        do_raw = sb.tile([P, PACK, NQ], F32, name="do_raw", align_bytes=DMA_ALIGN)
+        qm_raw = [sb.tile([P, PACK, P], F32, name=f"qm_raw{c}", align_bytes=DMA_ALIGN) for c in range(2)]
+        p_half = [sb.tile([P, PACK, HALF], F32, name=f"p_half{h}", align_bytes=DMA_ALIGN) for h in range(2)]
         delta_raw = sb.tile([P, PACK], F32, name="delta_raw")
-        windows = [sb.tile([P, T], F32, name=f"window{c}") for c in range(2)]
+        windows = [sb.tile([P, T], F32, name=f"window{c}", align_bytes=DMA_ALIGN) for c in range(2)]
 
         def slots(first, width):
             return offsets[:, first // 16 : (first + width) // 16]
@@ -66,8 +68,8 @@ def tile_attend_bwd_kernel(tc, doT, v_words, v_scales, p, delta, qm, offs, out):
         qm_rows = qm[0].rearrange("(p t) d -> p t d", t=PACK)
         nc.sync.dma_start(qm_raw[0][:], qm_rows[:, :, 0:P])
         nc.sync.dma_start(p_half[0][:], p_rows[:, :, 0:HALF])
-        nc.sync.dma_start(p_half[1][:], p_rows[:, :, HALF:N])
         nc.sync.dma_start(qm_raw[1][:], qm_rows[:, :, P:D])
+        nc.sync.dma_start(p_half[1][:], p_rows[:, :, HALF:N])
 
         warm = sb.tile([P, 2], F32, name="warm")
         nc.vector.memset(warm[:, 0:1], 0.0)
@@ -80,7 +82,7 @@ def tile_attend_bwd_kernel(tc, doT, v_words, v_scales, p, delta, qm, offs, out):
 
         do_codes, do_scales = [], []
         do_by_u = do_raw[:].rearrange("p j (m u w) -> p u m j w", u=2, w=2)
-        do_bf = [sb.tile([P, 2, P, PACK], BF16, name=("pool_scales", "do_bf1")[u], align_bytes=64) for u in range(2)]
+        do_bf = [sb.tile([P, 2, P, PACK], BF16, name=("pool_scales", "do_bf1")[u], align_bytes=DMA_ALIGN) for u in range(2)]
         nc.vector.tensor_copy(do_bf[0][:].rearrange("p w m j -> p m j w"), do_by_u[:, 0])
         nc.scalar.copy(do_bf[1][:].rearrange("p w m j -> p m j w"), do_by_u[:, 1])
         for u in range(2):
@@ -96,7 +98,7 @@ def tile_attend_bwd_kernel(tc, doT, v_words, v_scales, p, delta, qm, offs, out):
         banks = [ps.tile([P, N], F32, name=f"bank{b}") for b in range(8)]
         gathered = []
         for a, (first, width) in enumerate([(0, PIECE), (PIECE, PIECE), (HALF, HALF)]):
-            sel = sb.tile([P, width], U32, name=("pool_scales", "do_bf1", "sel2")[a], align_bytes=64)
+            sel = sb.tile([P, width], U32, name=("pool_scales", "do_bf1", "sel2")[a], align_bytes=DMA_ALIGN)
             nc.vector.tensor_copy(sel[:], pool_words[:].bitcast(U32).indirect(slots(first, width)))
             gathered.append(sel)
 
@@ -124,7 +126,7 @@ def tile_attend_bwd_kernel(tc, doT, v_words, v_scales, p, delta, qm, offs, out):
         qm_bf0 = sb.tile([P, P, PACK], BF16, name="qm_bf0", align_bytes=64)[:]
         ds_codes = sb.tile([P, N], U32, name="ds_codes", align_bytes=64)
         ds_scales = sb.tile([P, N], U8, name="ds_scales", align_bytes=64)
-        qm_codes = [sb.tile([P, P], U32, name=f"qm_codes{c}", align_bytes=64) for c in range(2)]
+        qm_codes = [sb.tile([P, P], U32, name="qm_codes0", align_bytes=64)[:]]
         qm_scales = [sb.tile([P, P], U8, name=f"qm_scales{c}", align_bytes=64) for c in range(2)]
 
         def weigh(words, centred_rows, p_rows_sb):
@@ -137,7 +139,7 @@ def tile_attend_bwd_kernel(tc, doT, v_words, v_scales, p, delta, qm, offs, out):
             acc = banks[bank_no][:, 0:width]
             nc.tensor.matmul_mx(
                 acc,
-                lhsT=qm_codes[c][:].bitcast(FP8X4),
+                lhsT=qm_codes[c].bitcast(FP8X4),
                 lhsT_scale=qm_scales[c][:],
                 rhs=ds_codes[:, first : first + width].bitcast(FP8X4),
                 rhs_scale=ds_scales[:, first : first + width],
@@ -147,22 +149,24 @@ def tile_attend_bwd_kernel(tc, doT, v_words, v_scales, p, delta, qm, offs, out):
             return acc
 
         nc.vector.tensor_copy(interleaved(qm_bf0), in_runs(qm_raw[0][:]))
-        quantize(qm_codes[0][:], qm_scales[0][:], qm_bf0)
+        quantize(qm_codes[0], qm_scales[0][:], qm_bf0)
         centred = [sb.tile([P, PACK, PIECE], F32, name=f"centred{a}", align_bytes=64) for a in range(2)]
         for a in range(2):
             for t in range(PACK):
                 centre(centred[a], t, dp_product(gathered[a], a * PIECE, PIECE, t, PACK * a + t))
-        centred_late = sb.tile([P, PACK, HALF], F32, name="centred_late")
-        for t in range(PACK):
-            centre(centred_late, t, dp_product(gathered[2], HALF, HALF, t, t))
+        centred_late = [sb.tile([P, PACK, PIECE], F32, name=f"centred_late{a}", align_bytes=64) for a in range(2)]
+        late_banks = [dp_product(gathered[2], HALF, HALF, t, t) for t in range(PACK)]
+        for a in range(2):
+            for t in range(PACK):
+                centre(centred_late[a], t, late_banks[t][:, a * PIECE : (a + 1) * PIECE])
 
         for a in range(2):
             weigh(ds_bf[a], centred[a][:], p_half[0][:, :, a * PIECE : (a + 1) * PIECE])
         for a in range(2):
             quantize_ds(a * PIECE, PIECE, ds_bf[a])
         qm_bf1 = sb.tile([P, P, PACK], BF16, name="centred0", align_bytes=64)
-        nc.scalar.copy(interleaved(qm_bf1[:, 0 : P // 2, :]), in_runs(qm_raw[1][:, :, 0 : P // 2]))
-        nc.vector.tensor_copy(interleaved(qm_bf1[:, P // 2 : P, :]), in_runs(qm_raw[1][:, :, P // 2 : P]))
+        nc.scalar.copy(interleaved(qm_bf1[:, 0:QM_SHARE, :]), in_runs(qm_raw[1][:, :, 0:QM_SHARE]))
+        nc.vector.tensor_copy(interleaved(qm_bf1[:, QM_SHARE:P, :]), in_runs(qm_raw[1][:, :, QM_SHARE:P]))
         dk0 = [sb.tile([P, HALF], F32, name=f"dk0{h}") for h in range(2)]
         for a in range(2):
             nc.scalar.copy(dk0[0][:, a * PIECE : (a + 1) * PIECE], dk_product(0, a * PIECE, PIECE, PACK + a))
@@ -170,19 +174,20 @@ def tile_attend_bwd_kernel(tc, doT, v_words, v_scales, p, delta, qm, offs, out):
 
         pieces = [slice(a * PIECE, (a + 1) * PIECE) for a in range(2)]
         late_bf = [sb.tile([P, PIECE, PACK], BF16, name=tag, align_bytes=64)[:] for tag in ("ds_bf0", "ds_bf1")]
-        weigh(late_bf[0], centred_late[:, :, pieces[0]], p_half[1][:, :, pieces[0]])
-        quantize(qm_codes[1][:], qm_scales[1][:], qm_bf1[:])
-        weigh(late_bf[1], centred_late[:, :, pieces[1]], p_half[1][:, :, pieces[1]])
+        weigh(late_bf[0], centred_late[0][:], p_half[1][:, :, pieces[0]])
+        weigh(late_bf[1], centred_late[1][:], p_half[1][:, :, pieces[1]])
         for a in range(2):
             quantize_ds(HALF + a * PIECE, PIECE, late_bf[a])
-        dk1_all = sb.tile([P, N], F32, name="dk1_all")
-        nc.vector.tensor_copy(dk1_all[:, 0:HALF], dk_product(1, 0, HALF, 0))
+        qm_codes.append(sb.tile([P, P], U32, name="centred_late1", align_bytes=64)[:])
+        quantize(qm_codes[1], qm_scales[1][:], qm_bf1[:])
         for a, cols in enumerate(pieces):
             nc.vector.tensor_copy(dk0[1][:, cols], dk_product(0, HALF + a * PIECE, PIECE, 6 + a))
         nc.scalar.activation(windows[0][:].indirect(slots(HALF, HALF)), dk0[1][:], COPY)
-        nc.sync.dma_start(out[0:P, :], windows[0][:])
+        nc.scalar.dma_start(out[0:P, :], windows[0][:])
 
-        nc.vector.tensor_copy(dk1_all[:, HALF:N], dk_product(1, HALF, HALF, 1))
+        dk1_all = sb.tile([P, N], F32, name="dk1_all")
+        for h in range(2):
+            nc.vector.tensor_copy(dk1_all[:, h * HALF : (h + 1) * HALF], dk_product(1, h * HALF, HALF, h))
         for h in range(2):
             nc.vector.tensor_copy(windows[1][:].indirect(slots(h * HALF, HALF)), dk1_all[:, h * HALF : (h + 1) * HALF])
         nc.sync.dma_start(out[P : 2 * P, :], windows[1][:])

@@ -21,7 +21,7 @@ PACK = 4
 DMA_ALIGN = 256
 HALF = N // 2
 PIECE = HALF // 2
-QM_SHARE = 32
+QM_SHARE = 64
 LIST_COLS = N // 16
 SCALE_WORDS = T // 4
 RUN = 4
@@ -164,9 +164,8 @@ def tile_attend_bwd_kernel(tc, doT, v_words, v_scales, p, delta, qm, offs, out):
             weigh(ds_bf[a], centred[a][:], p_half[0][:, :, a * PIECE : (a + 1) * PIECE])
         for a in range(2):
             quantize_ds(a * PIECE, PIECE, ds_bf[a])
-        qm_bf1 = sb.tile([P, P, PACK], BF16, name="centred0", align_bytes=64)
-        nc.scalar.copy(interleaved(qm_bf1[:, 0:QM_SHARE, :]), in_runs(qm_raw[1][:, :, 0:QM_SHARE]))
-        nc.vector.tensor_copy(interleaved(qm_bf1[:, QM_SHARE:P, :]), in_runs(qm_raw[1][:, :, QM_SHARE:P]))
+        qm_bf1 = [sb.tile([P, QM_SHARE, PACK], BF16, name="centred0", align_bytes=64)]
+        nc.vector.tensor_copy(interleaved(qm_bf1[0][:]), in_runs(qm_raw[1][:, :, 0:QM_SHARE]))
         dk0 = [sb.tile([P, HALF], F32, name=f"dk0{h}") for h in range(2)]
         for a in range(2):
             nc.scalar.copy(dk0[0][:, a * PIECE : (a + 1) * PIECE], dk_product(0, a * PIECE, PIECE, PACK + a))
@@ -176,10 +175,14 @@ def tile_attend_bwd_kernel(tc, doT, v_words, v_scales, p, delta, qm, offs, out):
         late_bf = [sb.tile([P, PIECE, PACK], BF16, name=tag, align_bytes=64)[:] for tag in ("ds_bf0", "ds_bf1")]
         weigh(late_bf[0], centred_late[0][:], p_half[1][:, :, pieces[0]])
         weigh(late_bf[1], centred_late[1][:], p_half[1][:, :, pieces[1]])
+        qm_bf1.append(sb.tile([P, QM_SHARE, PACK], BF16, name="centred_late0", align_bytes=64))
+        nc.vector.tensor_copy(interleaved(qm_bf1[1][:]), in_runs(qm_raw[1][:, :, QM_SHARE:P]))
         for a in range(2):
             quantize_ds(HALF + a * PIECE, PIECE, late_bf[a])
         qm_codes.append(sb.tile([P, P], U32, name="centred_late1", align_bytes=64)[:])
-        quantize(qm_codes[1], qm_scales[1][:], qm_bf1[:])
+        for a in range(2):
+            cols = slice(a * QM_SHARE, (a + 1) * QM_SHARE)
+            quantize(qm_codes[1][:, cols], qm_scales[1][:, cols], qm_bf1[a][:])
         for a, cols in enumerate(pieces):
             nc.vector.tensor_copy(dk0[1][:, cols], dk_product(0, HALF + a * PIECE, PIECE, 6 + a))
         nc.scalar.activation(windows[0][:].indirect(slots(HALF, HALF)), dk0[1][:], COPY)

@@ -96,11 +96,20 @@ def tile_attend_bwd_kernel(tc, doT, v_words, v_scales, p, delta, qm, offs, out):
         nc.scalar.mul(minus_delta[:], delta_raw[:], -1.0)
 
         banks = [ps.tile([P, N], F32, name=f"bank{b}") for b in range(8)]
-        gathered = []
-        for a, (first, width) in enumerate([(0, PIECE), (PIECE, PIECE), (HALF, HALF)]):
-            sel = sb.tile([P, width], U32, name=("pool_scales", "do_bf1", "sel2")[a], align_bytes=DMA_ALIGN)
-            nc.vector.tensor_copy(sel[:], pool_words[:].bitcast(U32).indirect(slots(first, width)))
-            gathered.append(sel)
+        gathered = [
+            sb.tile([P, width], U32, name=tag, align_bytes=DMA_ALIGN)
+            for width, tag in ((PIECE, "pool_scales"), (PIECE, "do_bf1"), (HALF, "sel2"))
+        ]
+
+        def gather(sel, first, width):
+            nc.vector.tensor_copy(sel, pool_words[:].bitcast(U32).indirect(slots(first, width)))
+
+        qm_bf0 = sb.tile([P, P, PACK], BF16, name="qm_bf0", align_bytes=64)[:]
+        gather(gathered[0][:], 0, PIECE)
+        gather(gathered[1][:], PIECE, PIECE)
+        gather(gathered[2][:, 0:PIECE], HALF, PIECE)
+        nc.vector.tensor_copy(interleaved(qm_bf0), in_runs(qm_raw[0][:]))
+        gather(gathered[2][:, PIECE:HALF], HALF + PIECE, PIECE)
 
         def dp_product(words, first, width, t, bank_no):
             u, w = divmod(t, 2)
@@ -123,7 +132,6 @@ def tile_attend_bwd_kernel(tc, doT, v_words, v_scales, p, delta, qm, offs, out):
             nc.vector.quantize_mx(codes.bitcast(FP8X4), scales, words.rearrange("p n t -> p (n t)"))
 
         ds_bf = [sb.tile([P, PIECE, PACK], BF16, name=f"ds_bf{a}", align_bytes=64)[:] for a in range(2)]
-        qm_bf0 = sb.tile([P, P, PACK], BF16, name="qm_bf0", align_bytes=64)[:]
         ds_codes = sb.tile([P, N], U32, name="ds_codes", align_bytes=64)
         ds_scales = sb.tile([P, N], U8, name="ds_scales", align_bytes=64)
         qm_codes = [sb.tile([P, P], U32, name="qm_codes0", align_bytes=64)[:]]
@@ -148,7 +156,6 @@ def tile_attend_bwd_kernel(tc, doT, v_words, v_scales, p, delta, qm, offs, out):
             )
             return acc
 
-        nc.vector.tensor_copy(interleaved(qm_bf0), in_runs(qm_raw[0][:]))
         quantize(qm_codes[0], qm_scales[0][:], qm_bf0)
         centred = [sb.tile([P, PACK, PIECE], F32, name=f"centred{a}", align_bytes=64) for a in range(2)]
         for a in range(2):

@@ -74,7 +74,8 @@ def tile_attend_bwd_kernel(tc, doT, v_words, v_scales, p, delta, qm, offs, out):
         warm = sb.tile([P, 2], F32, name="warm")
         nc.vector.memset(warm[:, 0:1], 0.0)
         nc.scalar.copy(warm[:, 1:2], warm[:, 0:1])
-        nc.vector.memset(windows[0][:].bitcast(I32), 0)
+        for cols in (slice(0, T // 2 - 1), slice(T // 2 - 1, T)):
+            nc.vector.memset(windows[0][:].bitcast(I32)[:, cols], 0)
         nc.gpsimd.memset(windows[1][:].bitcast(I32), 0)
 
         v_sel_scales = sb.tile([P, N], U8, name="v_sel_scales", align_bytes=64)

from contextlib import ExitStack

import concourse.mybir as mybir

NQ, N, T, D, DV = 512, 512, 2048, 256, 512
FLOPS = 2 * DV * NQ * N + 2 * NQ * D * N

F32 = mybir.dt.float32
BF16 = mybir.dt.bfloat16
I32 = mybir.dt.int32
U32 = mybir.dt.uint32
U16 = mybir.dt.uint16
U8 = mybir.dt.uint8
FP8X4 = mybir.dt.float8_e4m3fn_x4
MULT = mybir.AluOpType.mult
IDENTITY = mybir.ActivationFunctionType.Identity
COPY = mybir.ActivationFunctionType.Copy

P = 128
PACK = 4
DMA_ALIGN = 256
HALF = N // 2
PIECE = HALF // 2
QM_SHARE = 64
LIST_COLS = N // 16
SCALE_WORDS = T // 4
RUN = 4


def in_runs(rows):
    return rows.rearrange("p t (c i) -> p c t i", i=RUN)


def interleaved(words):
    return words.rearrange("p (c i) t -> p c t i", i=RUN)


def tile_attend_bwd_kernel(tc, doT, v_words, v_scales, p, delta, qm, offs, out):
    nc = tc.nc
    with ExitStack() as ctx:
        sb = ctx.enter_context(tc.tile_pool(name="sb", bufs=1))
        ps = ctx.enter_context(tc.psum_pool(name="ps", bufs=1))

        offsets = sb.tile([P, LIST_COLS], U16, name="offsets")
        pool_scales = sb.tile([P, SCALE_WORDS], I32, name="pool_scales", align_bytes=DMA_ALIGN)
        pool_words = sb.tile([P, T], I32, name="pool_words", align_bytes=DMA_ALIGN)
        do_raw = sb.tile([P, PACK, NQ], F32, name="do_raw", align_bytes=DMA_ALIGN)
        qm_raw = [sb.tile([P, PACK, P], F32, name=f"qm_raw{c}", align_bytes=DMA_ALIGN) for c in range(2)]
        p_half = [sb.tile([P, PACK, HALF], F32, name=f"p_half{h}", align_bytes=DMA_ALIGN) for h in range(2)]
        delta_raw = sb.tile([P, PACK], F32, name="delta_raw")
        windows = [sb.tile([P, T], F32, name=f"window{c}", align_bytes=DMA_ALIGN) for c in range(2)]

        def slots(first, width):
            return offsets[:, first // 16 : (first + width) // 16]

        nc.gpsimd.memset(pool_scales[:], 0)

        do_rows = doT[0].rearrange("(p j) q -> p j q", j=PACK)
        nc.sync.dma_start(do_raw[:, 0:2, :], do_rows[:, 0:2, :])
        nc.sync.dma_start(offsets[:], offs)
        scale_rows = v_scales[0].bitcast(I32)
        for r in range(4):
            nc.sync.dma_start(pool_scales[r:P:32, :], scale_rows[r:16:4, :])
        nc.sync.dma_start(do_raw[:, 2:4, :], do_rows[:, 2:4, :])
        nc.sync.dma_start(pool_words[:], v_words[0].rearrange("p n r -> p (n r)").bitcast(I32))
        nc.sync.dma_start(delta_raw[:], delta[0].rearrange("(p t) o -> p (t o)", t=PACK))
        p_rows = p[0].rearrange("(p t) n -> p t n", t=PACK)
        qm_rows = qm[0].rearrange("(p t) d -> p t d", t=PACK)
        nc.sync.dma_start(qm_raw[0][:], qm_rows[:, :, 0:P])
        nc.sync.dma_start(p_half[0][:], p_rows[:, :, 0:HALF])
        nc.sync.dma_start(qm_raw[1][:], qm_rows[:, :, P:D])
        nc.sync.dma_start(p_half[1][:], p_rows[:, :, HALF:N])

        warm = sb.tile([P, 2], F32, name="warm")
        nc.vector.memset(warm[:, 0:1], 0.0)
        nc.scalar.copy(warm[:, 1:2], warm[:, 0:1])
        for cols in (slice(0, T // 2 - 1), slice(T // 2 - 1, T)):
            nc.vector.memset(windows[0][:].bitcast(I32)[:, cols], 0)
        nc.gpsimd.memset(windows[1][:].bitcast(I32), 0)

        v_sel_scales = sb.tile([P, N], U8, name="v_sel_scales", align_bytes=64)
        nc.vector.tensor_copy(v_sel_scales[:], pool_scales[:].bitcast(U8).indirect(offsets[:]))

        do_codes, do_scales = [], []
        do_by_u = do_raw[:].rearrange("p j (m u w) -> p u m j w", u=2, w=2)
        do_bf = [sb.tile([P, 2, P, PACK], BF16, name=("pool_scales", "do_bf1")[u], align_bytes=DMA_ALIGN) for u in range(2)]
        nc.vector.tensor_copy(do_bf[0][:].rearrange("p w m j -> p m j w"), do_by_u[:, 0])
        nc.scalar.copy(do_bf[1][:].rearrange("p w m j -> p m j w"), do_by_u[:, 1])
        for u in range(2):
            codes = sb.tile([P, 2 * P], U32, name=f"do_codes{u}", align_bytes=64)
            scales = sb.tile([P, 2 * P], U8, name=f"do_scales{u}", align_bytes=64)
            nc.vector.quantize_mx(codes[:].bitcast(FP8X4), scales[:], do_bf[u][:].rearrange("p w m j -> p (w m j)"))
            do_codes.append(codes)
            do_scales.append(scales)

        minus_delta = sb.tile([P, PACK], F32, name="minus_delta")
        nc.scalar.mul(minus_delta[:], delta_raw[:], -1.0)

        banks = [ps.tile([P, N], F32, name=f"bank{b}") for b in range(8)]
        gathered = [
            sb.tile([P, width], U32, name=tag, align_bytes=DMA_ALIGN)
            for width, tag in ((PIECE, "pool_scales"), (PIECE, "do_bf1"), (HALF, "sel2"))
        ]

        def gather(sel, first, width):
            nc.vector.tensor_copy(sel, pool_words[:].bitcast(U32).indirect(slots(first, width)))

        qm_bf0 = sb.tile([P, P, PACK], BF16, name="qm_bf0", align_bytes=64)[:]
        gather(gathered[0][:], 0, PIECE)
        gather(gathered[1][:], PIECE, PIECE)
        gather(gathered[2][:, 0:PIECE], HALF, PIECE)
        nc.vector.tensor_copy(interleaved(qm_bf0), in_runs(qm_raw[0][:]))
        gather(gathered[2][:, PIECE:HALF], HALF + PIECE, PIECE)

        def dp_product(words, first, width, t, bank_no):
            u, w = divmod(t, 2)
            bank = banks[bank_no][:, 0:width]
            nc.tensor.matmul_mx(
                bank,
                lhsT=do_codes[u][:, w * P : (w + 1) * P].bitcast(FP8X4),
                lhsT_scale=do_scales[u][:, w * P : (w + 1) * P],
                rhs=words[:].bitcast(FP8X4),
                rhs_scale=v_sel_scales[:, first : first + width],
                start=True,
                stop=True,
            )
            return bank

        def centre(rows, t, bank):
            nc.scalar.activation(rows[:, t, :], bank, IDENTITY, bias=minus_delta[:, t : t + 1])

        def quantize(codes, scales, words):
            nc.vector.quantize_mx(codes.bitcast(FP8X4), scales, words.rearrange("p n t -> p (n t)"))

        ds_bf = [sb.tile([P, PIECE, PACK], BF16, name=f"ds_bf{a}", align_bytes=64)[:] for a in range(2)]
        ds_codes = sb.tile([P, N], U32, name="ds_codes", align_bytes=64)
        ds_scales = sb.tile([P, N], U8, name="ds_scales", align_bytes=64)
        qm_codes = [sb.tile([P, P], U32, name="qm_codes0", align_bytes=64)[:]]
        qm_scales = [sb.tile([P, P], U8, name=f"qm_scales{c}", align_bytes=64) for c in range(2)]

        def weigh(words, centred_rows, p_rows_sb):
            nc.vector.tensor_tensor(interleaved(words), in_runs(centred_rows), in_runs(p_rows_sb), MULT)

        def quantize_ds(first, width, words):
            quantize(ds_codes[:, first : first + width], ds_scales[:, first : first + width], words)

        def dk_product(c, first, width, bank_no):
            acc = banks[bank_no][:, 0:width]
            nc.tensor.matmul_mx(
                acc,
                lhsT=qm_codes[c].bitcast(FP8X4),
                lhsT_scale=qm_scales[c][:],
                rhs=ds_codes[:, first : first + width].bitcast(FP8X4),
                rhs_scale=ds_scales[:, first : first + width],
                start=True,
                stop=True,
            )
            return acc

        quantize(qm_codes[0], qm_scales[0][:], qm_bf0)
        centred = [sb.tile([P, PACK, PIECE], F32, name=f"centred{a}", align_bytes=64) for a in range(2)]
        for a in range(2):
            for t in range(PACK):
                centre(centred[a], t, dp_product(gathered[a], a * PIECE, PIECE, t, PACK * a + t))
        centred_late = [sb.tile([P, PACK, PIECE], F32, name=f"centred_late{a}", align_bytes=64) for a in range(2)]
        late_banks = [dp_product(gathered[2], HALF, HALF, t, t) for t in range(PACK)]
        for a in range(2):
            for t in range(PACK):
                centre(centred_late[a], t, late_banks[t][:, a * PIECE : (a + 1) * PIECE])

        for a in range(2):
            weigh(ds_bf[a], centred[a][:], p_half[0][:, :, a * PIECE : (a + 1) * PIECE])
        for a in range(2):
            quantize_ds(a * PIECE, PIECE, ds_bf[a])
        qm_bf1 = [sb.tile([P, QM_SHARE, PACK], BF16, name="centred0", align_bytes=64)]
        nc.vector.tensor_copy(interleaved(qm_bf1[0][:]), in_runs(qm_raw[1][:, :, 0:QM_SHARE]))
        dk0 = [sb.tile([P, HALF], F32, name=f"dk0{h}") for h in range(2)]
        for a in range(2):
            nc.scalar.copy(dk0[0][:, a * PIECE : (a + 1) * PIECE], dk_product(0, a * PIECE, PIECE, PACK + a))
        nc.scalar.activation(windows[0][:].indirect(slots(0, HALF)), dk0[0][:], COPY)

        pieces = [slice(a * PIECE, (a + 1) * PIECE) for a in range(2)]
        late_bf = [sb.tile([P, PIECE, PACK], BF16, name=tag, align_bytes=64)[:] for tag in ("ds_bf0", "ds_bf1")]
        weigh(late_bf[0], centred_late[0][:], p_half[1][:, :, pieces[0]])
        weigh(late_bf[1], centred_late[1][:], p_half[1][:, :, pieces[1]])
        qm_bf1.append(sb.tile([P, QM_SHARE, PACK], BF16, name="centred_late0", align_bytes=64))
        nc.vector.tensor_copy(interleaved(qm_bf1[1][:]), in_runs(qm_raw[1][:, :, QM_SHARE:P]))
        for a in range(2):
            quantize_ds(HALF + a * PIECE, PIECE, late_bf[a])
        qm_codes.append(sb.tile([P, P], U32, name="centred_late1", align_bytes=64)[:])
        for a in range(2):
            cols = slice(a * QM_SHARE, (a + 1) * QM_SHARE)
            quantize(qm_codes[1][:, cols], qm_scales[1][:, cols], qm_bf1[a][:])
        for a, cols in enumerate(pieces):
            nc.vector.tensor_copy(dk0[1][:, cols], dk_product(0, HALF + a * PIECE, PIECE, 6 + a))
        nc.scalar.activation(windows[0][:].indirect(slots(HALF, HALF)), dk0[1][:], COPY)
        nc.scalar.dma_start(out[0:P, :], windows[0][:])

        dk1_all = sb.tile([P, N], F32, name="dk1_all")
        for h in range(2):
            nc.vector.tensor_copy(dk1_all[:, h * HALF : (h + 1) * HALF], dk_product(1, h * HALF, HALF, h))
        for h in range(2):
            nc.vector.tensor_copy(windows[1][:].indirect(slots(h * HALF, HALF)), dk1_all[:, h * HALF : (h + 1) * HALF])
        nc.sync.dma_start(out[P : 2 * P, :], windows[1][:])
